import numpy as np, ml_dtypes
CORES = [1,5,17,21,33,37,49,53]
N = 8
BF = ml_dtypes.bfloat16
def gentries(a):
    return np.ascontiguousarray(a.reshape(8, 16, -1).transpose(0, 2, 1)).reshape(8, -1)
def gtable(e):
    e = np.asarray(e); return np.ascontiguousarray(e.reshape(8, -1, 16).transpose(0, 2, 1)).reshape(128, -1).astype(np.int32)
V, S, L, M, C, A, B = 3072, 1024, 3, 3, 192, 5, 32
W = V + C * M
def parts(rng):
    c = rng.integers(0, 16, (N, 8, 12, V)); o = np.argsort(rng.random((N, 8, 1, V)), axis=-1)
    i = np.minimum((V * rng.random((N, 8, 2, V)) ** 1.5).astype(np.int64), V - 1)
    t = np.take_along_axis(np.broadcast_to(o, (N, 8, 2, V)), i, 3)
    t = np.where(rng.random(t.shape) < 0.04, np.arange(V), t)
    n = np.exp2(9 * rng.random((N, 8, 2, V))).astype(np.int64) - 1
    s = rng.integers(0, V, (N, 8, S)); x = rng.integers(0, 16, (N, 8, 12, S))
    e = np.where(np.argsort(rng.random((N, 8, 12)), axis=-1) % 2 == 1, 1, -1)
    return c, t, n, s, x, e
def pack(c, t, n, s, x, e):
    return {"recs": np.concatenate([c, t, n], axis=2).reshape(N, 128, V).astype(np.int32), "st0": np.stack([gtable(a) for a in s]),
            "cx0": np.concatenate([x, np.zeros((N, 8, 4, S), np.int64)], axis=2).reshape(N, 128, S).astype(np.float32).astype(BF),
            "sg": np.concatenate([e, np.zeros((N, 8, 4), np.int64)], axis=2).reshape(N, 128, 1).astype(np.int32)}
def setup_inputs(rng):
    return pack(*parts(rng))
def setup_inputs_full(rng):
    c, t, n, s, x, e = parts(rng); n = rng.integers(400, 501, n.shape); h = V // M
    for g in range(8):
        base = rng.permutation(V)
        for r in range(N):
            for m in range(M):
                blk = rng.permutation(base[m * h:(m + 1) * h])
                t[r, g][:, blk] = np.roll(blk, -1)
                s[r, g, m * C:(m + 1) * C] = blk[:C] if g % 2 == 0 else rng.permutation(blk)[:C]
    return pack(c, t, n, s, x, e)
def setup_inputs_meet(rng):
    c, t, n, s, x, e = parts(rng); n = n // 4 + 60
    hub = np.stack([rng.permutation(V)[:24] for g in range(8)])
    t = np.where(rng.random(t.shape) < 0.85, hub[np.arange(8)[None, :, None, None], rng.integers(0, 24, t.shape)], t)
    for r in range(N):
        for g in range(8): t[r, g][:, hub[g, :6]] = hub[g, :6]
    s[:, 0] = s[:, 0, :1].copy(); x[:, 0] = x[:, 0, :, :1].copy(); t[:, 1] = np.arange(V)
    for r in range(N):
        o = rng.permutation(V); h = o[L * C]
        t[r, 4][:, o[:(L - 1) * C]] = o[C:L * C]; t[r, 4][:, o[(L - 1) * C:L * C]] = h
        n[r, 4][:, h] = rng.integers(400, 501, 2); s[r, 4, :C] = rng.permutation(o[:C])
    return pack(c, t, n, s, x, e)
def setup_inputs_ties(rng):
    c, t, n, s, x, e = parts(rng); c[:, ::2] = c[:, ::2] & 1; x[:, ::2] = x[:, ::2] & 1
    a = A - 2 + rng.integers(0, 4, (N, 8, V)); b = A - 2 + rng.integers(0, 4, (N, 8, V))
    b = np.where(rng.random((N, 8, V)) < 0.6, A + B - a + rng.integers(-3, 4, (N, 8, V)), b)
    turn = rng.random((N, 8, V)) < 0.5
    n = np.stack([np.where(turn, b, a), np.where(turn, a, b)], axis=2)
    o = np.argsort(rng.random((N, 8, 1, V)), axis=-1)[..., :3 * C]
    t = np.take_along_axis(np.broadcast_to(o, (N, 8, 2, 3 * C)), rng.integers(0, 3 * C, t.shape), 3)
    return pack(c, t, n, s, x, e)
def setup_inputs_ahead(rng):
    c, t, n, s, x, e = parts(rng); n = rng.integers(300, 401, n.shape); n[1::2] = 0
    t[:, 2] = np.where(rng.random((N, 2, V)) < 0.5, (V - 1) * rng.integers(0, 2, (N, 2, V)), t[:, 2])
    s[:, 3] = (V - 1) * rng.integers(0, 2, (N, S))
    return pack(c, t, n, s, x, e)
def setup_inputs_spread(rng):
    c, t, n, s, x, e = parts(rng)
    c = np.minimum((np.exp2(4 * rng.random((N, 8, 1, V))) * rng.random((N, 8, 12, V))).astype(np.int64), 15); c[rng.random(c.shape) < 0.02] = 15
    x = np.minimum((np.exp2(4 * rng.random((N, 8, 1, S))) * rng.random((N, 8, 12, S))).astype(np.int64), 15)
    t = np.minimum((V * rng.random(t.shape) ** np.exp2(rng.integers(-1, 3, (N, 8, 1, 1)))).astype(np.int64), V - 1)
    n = np.minimum(np.exp2(12 * rng.random(n.shape)).astype(np.int64), 4095); n[rng.random(n.shape) < 0.1] = 0; n[rng.random(n.shape) < 0.01] = 4095
    e = np.where(rng.random(e.shape) < 0.5, 1, -1); e[:, 1] = 1; e[:, 6] = -1
    for g, a in ((2, 1), (5, -1)): e[:, g] = np.where(np.argsort(rng.random((N, 12)), axis=-1) < 10, a, -a)
    for g in (1, 2, 5, 6):
        c[:, g] = np.where(rng.random((N, 1, V)) < 0.5, rng.integers(14, 16, (N, 12, V)), c[:, g])
        x[:, g] = np.where(rng.random((N, 1, S)) < 0.5, rng.integers(14, 16, (N, 12, S)), x[:, g])
    n[:, 3] = rng.integers(4000, 4096, (N, 2, V))
    return pack(c, t, n, s, x, e)
def check_inputs(d):
    bad = []
    a = np.asarray(d["recs"]).reshape(-1, 8, 16, V)
    for k, i, j, hi in (("statistics", 0, 12, 15), ("transitions", 12, 14, V - 1), ("counts", 14, 16, 4095)):
        if np.min(a[:, :, i:j]) < 0 or np.max(a[:, :, i:j]) > hi: bad.append("range of the " + k)
    if np.min(d["st0"]) < 0 or np.max(d["st0"]) > V - 1: bad.append("range of st0")
    x = np.asarray(d["cx0"]).astype(np.float32).reshape(-1, 8, 16, S)
    if not np.all((x >= 0) & (x <= 15) & (x == np.floor(x))): bad.append("cx0 holds whole numbers from 0 to 15")
    if np.any(x[:, :, 12:] != 0): bad.append("rows of 0 of cx0")
    e = np.asarray(d["sg"]).reshape(-1, 8, 16)
    if not np.all(np.abs(e[:, :, :12]) == 1): bad.append("sg holds 1 and -1")
    if np.any(e[:, :, 12:] != 0): bad.append("rows of 0 of sg")
    return bad
def reference(recs, st0, cx0, sg):
    p = np.zeros((N, 8, 16, W), np.int64); p[..., :V] = recs.astype(np.int64).reshape(N, 8, 16, V)
    s = np.stack([gentries(a) for a in st0]).astype(np.int64)
    x = cx0.astype(np.float32).astype(np.int64).reshape(N, 8, 16, S)[:, :, :12].copy()
    e = sg.astype(np.int64).reshape(N, 8, 16, 1)[:, :, :12]
    free = np.full((N, 8), V, np.int64)
    for v in range(M):
        for q in range(N):
            r = (q - v) % N
            for step in range(L):
                rec = np.take_along_axis(p[q], s[r][:, None, :], 2)
                b = (np.sum(e[q] * rec[:, :12] * x[r], axis=1) > 0).astype(np.int64)
                x[r] = (x[r] + rec[:, :12]) >> 1
                old = s[r].copy(); s[r] = np.where(b == 1, rec[:, 13], rec[:, 12])
            lo = C * v
            for g in range(8):
                pg = p[q, g]; so = old[g, lo:lo + C]; bo = b[g, lo:lo + C]; sn = s[r, g, lo:lo + C].copy()
                w = np.sort(np.unique(so, return_index=True)[1])
                pg[14 + bo[w], so[w]] += 1
                w = w[np.sort(np.unique(sn[w], return_index=True)[1])]
                n = pg[14 + bo[w], so[w]]
                ok = (sn[w] != so[w]) & (n >= A) & (pg[14, sn[w]] + pg[15, sn[w]] - n >= B)
                w = w[ok]; k = len(w); new = free[q, g] + np.arange(k)
                t = pg[:, sn[w]]
                pg[:12, new] = (t[:12] + x[r, g][:, lo + w]) >> 1
                pg[12:14, new] = t[12:14]
                pg[14:16, new] = t[14:16] >> 1
                pg[14:16, sn[w]] = t[14:16] - (t[14:16] >> 1)
                pg[12 + bo[w], so[w]] = new
                s[r, g, lo + w] = new; free[q, g] += k
    yx = np.zeros((N, 8, 16, S), np.float32); yx[:, :, :12] = x
    return {"yp": p.reshape(N, 128, W).astype(np.float32), "ys": np.stack([gtable(a) for a in s]).astype(np.float32), "yx": yx.reshape(N, 128, S).astype(BF)}

@@ -1,0 +1,550 @@
+from concourse.mybir import AluOpType as A, ActivationFunctionType as F
+
+V, S, C, W = 3072, 1024, 192, 3648
+BASE = 384
+K, BIG, K2, MAG = 8192.0, 4096.0, 2048.0, 12582912.0
+CH = [(0, 192), (192, 416), (608, 416)]
+BFW = ["x", "x2", "y", "b", "sg", "win", "c", "s", "q", "qs", "tot"]
+F32W = ["i", "rs", "sr", "rt", "h"]
+
+SCRATCH = {
+    "raw": ("sbuf", [128, V], "int32"), "pool": ("sbuf", [128, BASE + W], "float32"),
+    "cnt2": ("sbuf", [128, BASE + W], "float32"), "ident": ("sbuf", [128, W], "float32"),
+    "sgi": ("sbuf", [128, 4], "int32"), "sti": ("sbuf", [128, 64], "int32"), "cxb": ("sbuf", [128, S], "bfloat16"),
+    "rec": ("sbuf", [128, S], "float32"), "pr": ("sbuf", [128, S], "float16"),
+    "wb": ("sbuf", [128, len(BFW), 8, 16], "bfloat16"), "wf": ("sbuf", [128, len(F32W), 8, 16], "float32"),
+    "wl": ("sbuf", [128, 144], "bfloat16"), "wz": ("sbuf", [128, 32], "float16"), "wr1": ("sbuf", [128, 8, 16], "float16"),
+    "ih": ("sbuf", [128, 128], "float16"), "bd": ("sbuf", [128, 8, 16], "bfloat16"),
+    "zero": ("sbuf", [128, 272], "bfloat16"), "half": ("sbuf", [128, C], "bfloat16"), "c16": ("sbuf", [128, 16], "float32"),
+    "pmi": ("sbuf", [128, 2], "int32"), "ki": ("sbuf", [128, 16], "float32"), "oh": ("sbuf", [128, 16], "float32"),
+    "oh2": ("sbuf", [128, 8], "float32"), "lt": ("sbuf", [128, 16], "float32"), "ww": ("sbuf", [128, 28], "float32"),
+    "col": ("sbuf", [128, 40], "float32"), "dum": ("sbuf", [128, 24], "float32"),
+    "thr": ("sbuf", [128, C], "bfloat16"), "d0": ("sbuf", [128, C], "bfloat16"),
+    "i1": ("sbuf", [128, 64], "uint16"), "i2": ("sbuf", [128, 64], "uint16"),
+    "sf": ("sbuf", [128, 12], "float32"), "tf": ("sbuf", [128, 12], "float32"), "tb": ("sbuf", [128, 12], "float32"),
+    "el1": ("sbuf", [128, 12], "float32"), "el2": ("sbuf", [128, 24], "float32"),
+    "srow": ("sbuf", [128, C], "float32"), "trow": ("sbuf", [128, C], "float32"),
+    "recs_": ("sbuf", [128, C], "float32"), "g2": ("sbuf", [128, C], "float32"),
+    "eb": ("sbuf", [128, 12, C], "bfloat16"), "sg1": ("sbuf", [128, C], "bfloat16"), "sgn": ("sbuf", [128, C], "bfloat16"),
+    "fl": ("sbuf", [128, C], "bfloat16"), "cr": ("sbuf", [128, 2, C], "bfloat16"),
+    "s1f": ("sbuf", [128, 12], "float32"), "wbig": ("sbuf", [128, 12], "float32"), "w1": ("sbuf", [128, 12], "float32"),
+    "si": ("sbuf", [128, 36], "uint16"), "idf": ("sbuf", [128, 24], "float32"), "ncf": ("sbuf", [128, 12], "float32"),
+    "bn": ("sbuf", [128, 3 * C], "float32"), "qn": ("sbuf", [128, 2 * C], "float32"), "hz": ("sbuf", [128, 2 * C], "float32"),
+    "inc": ("sbuf", [128, C], "float32"), "rr": ("sbuf", [128, C], "float32"),
+    "fs": ("sbuf", [128, 64], "float32"), "fland": ("sbuf", [128, 64], "float32"),
+    "xo": ("sbuf", [128, S], "bfloat16"), "xland": ("sbuf", [128, S], "bfloat16"),
+}
+for _v in range(3):
+    SCRATCH["y%d" % _v] = ("sbuf", [128, S], "bfloat16")
+    SCRATCH["ix%d" % _v] = ("sbuf", [128, 64], "uint16")
+    SCRATCH["io%d" % _v] = ("sbuf", [128, 64], "uint16")
+    SCRATCH["nc%d" % _v] = ("sbuf", [128, 12], "uint16")
+    SCRATCH["lz%d" % _v] = ("sbuf", [128, 34, 8], "float16")
+    SCRATCH["mk%d" % _v] = ("sbuf", [128, 128], "bfloat16")
+for _b in range(8):
+    SCRATCH["pb%d" % _b] = ("psum", [128, 512], "float32")
+
+N_DMA, N_ARR = 36, 20
+SEMAPHORES = (["c_pe", "c_act", "c_dve", "c_g", "sent"] + ["d%d" % i for i in range(N_DMA)]
+              + ["a%d" % i for i in range(N_ARR)])
+HOP = 120.0
+
+
+def build(T, topo, core, opt):
+    ops = []
+    CY, PCY, GA, SC, RL = opt["par"]
+    n = len(T.cores)
+    rank = T.rank_of(core)
+    cnt = {"d": 0, "a": 0}
+
+    def op(eng, fn, r, w, cost, banks=(), kind="c", lat=0.0, sem=None, inc=0):
+        ops.append(dict(eng=eng, fn=fn, r=list(r), w=list(w), cost=cost, banks=list(banks), kind=kind, lat=lat, sem=sem, inc=inc, lock=None))
+
+    def dve(fn, r, w, el, banks=()):
+        op("dve", fn, r, w, max(64, el) * CY, banks)
+
+    def act(fn, r, w, el, banks=()):
+        op("act", fn, r, w, max(64, el) * CY + 20, banks)
+
+    def pe(mms, r, w, banks):
+        def fn(e):
+            last = None
+            for m in mms:
+                last = e.matmul(m[0], m[1], m[2], m[3], m[4])
+            return last
+        op("pe", fn, r, w, sum(m[5] for m in mms) * PCY + 40, banks)
+
+    def dma(q, out, in_, r, w, nbytes):
+        sem = "d%d" % cnt["d"]; cnt["d"] += 1
+        op(q, lambda e: e.dma_start(out, in_), r, w, 60, kind="dma", lat=2000 + nbytes / 200.0, sem=sem, inc=16)
+
+    def send(step, out, in_, r, name, nbytes):
+        dst, src = T.cores[(rank + step) % n], T.cores[(rank - step) % n]
+        sem = "a%d" % cnt["a"]; cnt["a"] += 1
+        rid, pid, _ = topo.addr(dst)
+        m = topo.mask(core, dst)
+        op("g", lambda e: e.remote_dma(out, in_, T.sem[sem], T.sem.sent, pid, rid, m), r, ["arr:" + name], 400,
+           kind="rem", lat=RL + nbytes / 60.0, sem=sem, inc=len(topo.engines(src, core)))
+        ops[-1]["loc"] = len(topo.engines(core, dst))
+
+    wb = {k: T.wb[:, i] for i, k in enumerate(BFW)}
+    wf = {k: T.wf[:, i] for i, k in enumerate(F32W)}
+    cols = {}
+
+    def col(k):
+        if k not in cols:
+            cols[k] = len(cols)
+        return T.col[:, cols[k]:cols[k] + 1]
+
+    def oh(i):
+        return T.oh[:, i:i + 1]
+
+    def oh2(i):
+        return T.oh2[:, i:i + 1]
+
+    pw = T.pool[:, BASE:BASE + W]
+    pall = T.pool[:, 0:BASE + W]
+
+    lb_ = opt["loads"]
+    LOADS = len(lb_) - 1
+    dma("sp", T.sgi[:, 0:1], T.sg[:], [], ["sgi"], 512)
+    dma("act", T.sti[:], T.st0[:], [], ["sti"], 32768)
+    dma("act", T.cxb[:, 0:C], T.cx0[:, 0:C], [], ["cxb0"], 80000)
+    for i in range(LOADS):
+        dma("sp" if i % 2 == 0 else "act", T.raw[:, lb_[i]:lb_[i + 1]], T.recs[:, lb_[i]:lb_[i + 1]], [], ["raw%d" % i], 80000 + 512 * lb_[i + 1])
+    dma("sp", T.cxb[:, C:], T.cx0[:, C:], [], ["cxb1", "cxb2"], 1860000)
+    dve(lambda e: e.memset(T.bd[:], 1.0), [], ["bd"], 64)
+    dve(lambda e: e.memset(T.wb[:, 0:2], 0.0), [], ["wb_x", "wb_x2"], 128)
+    dve(lambda e: e.memset(T.wf[:, 0:1], 0.0), [], ["wf_i"], 128)
+    dve(lambda e: e.memset(T.wb[:, 2:], 0.0), [], ["wb_" + k for k in BFW[2:]], 64 * 9)
+    dve(lambda e: e.memset(T.wf[:, 1:], 0.0), [], ["wf_" + k for k in F32W[1:]], 128 * 5)
+    dve(lambda e: e.memset(T.wl[:], 0.0), [], ["wl"], 72)
+    dve(lambda e: e.memset(T.zero[:], 0.0), [], ["zero"], 136)
+    dve(lambda e: e.memset(T.half[:], 0.5), [], ["half"], 96)
+    dve(lambda e: e.memset(T.c16[:], 2.0 ** -16), [], ["c16"], 16)
+    dve(lambda e: e.memset(T.pool[:, 0:BASE], 0.0), [], ["poolA"], BASE)
+    dve(lambda e: e.memset(T.pool[:, BASE + V:], 0.0), [], ["poolB"], W - V)
+    dve(lambda e: e.memset(T.hz[:, 0:C], 0.0), [], ["hz0"], C)
+    dve(lambda e: e.memset(T.qn[:, C:], -1.0), [], ["qn1"], C)
+    dve(lambda e: e.memset(col("lb0"), V - 1 + BASE - BIG), [], ["lb0"], 1)
+
+    def gp(fn, r, w, el):
+        op("g", fn, r, w, 170 + 2 * el * 0.83)
+
+    gp(lambda e: e.iota(T.pmi[:, 0:1], [[0, 1]], 0, 1), [], ["pmi0"], 1)
+    gp(lambda e: e.iota(T.ki[:], [[1, 16]], 0, 0, allow_small_or_imprecise_dtypes=True), [], ["ki"], 16)
+    gp(lambda e: e.affine_select(T.bd[:], T.bd[:], [[-16, 8], [0, 16]], A.is_ge, 0.0, 0, 1), ["bd"], ["bd"], 128)
+    gp(lambda e: e.affine_select(T.bd[:], T.bd[:], [[16, 8], [0, 16]], A.is_ge, 0.0, 15, -1), ["bd"], ["bd"], 128)
+
+    def entry(buf, names, k, src, lo, hi, val, diag=False, step=1):
+        ap = T[buf][:, names.index(k), :, lo:hi:step]
+        m = len(range(lo, hi, step))
+        gp(lambda e: e.affine_select(ap, ap, [[-16, 8], [-1 if diag else 0, m]], A.not_equal, float(val), -src, 1),
+           [buf + "_" + k], [buf + "_" + k], 8 * m)
+
+    def eb_(*a, **kw):
+        entry("wb", BFW, *a, **kw)
+
+    def ef_(*a, **kw):
+        entry("wf", F32W, *a, **kw)
+
+    ef_("i", 0, 0, 16, 1.0, diag=True)
+    eb_("x", 0, 0, 12, 0.5, diag=True); eb_("x", 15, 0, 12, -0.5); eb_("x", 15, 12, 16, 1 / 256)
+    eb_("x2", 0, 0, 12, 0.5, diag=True); eb_("x2", 15, 0, 12, 255 / 512); eb_("x2", 15, 12, 16, 255 / 256)
+    idw = W // 8
+    gp(lambda e: e.iota(T.ident[:, 0:idw], [[1, idw]], 0, 0, allow_small_or_imprecise_dtypes=True), [], ["id0"], idw)
+    gp(lambda e: e.iota(T.dum[:], [[-C, 2], [16, 12]], C, 0, allow_small_or_imprecise_dtypes=True), [], ["dum"], 24)
+    for i, val in ((0, 1.0), (1, BIG)):
+        gp(lambda e, i=i, val=val: e.affine_select(T.wl[:, 15:143:16], T.wl[:, 15:143:16], [[-16, 8]], A.not_equal, val, -i, 1), ["wl"], ["wl"], 8)
+    ef_("rs", 14, 2, 4, 1.0, diag=True); ef_("rs", 14, 4, 6, -1.0, diag=True)
+    ef_("rs", 12, 6, 9, 1.0, diag=True, step=2); ef_("rs", 12, 7, 10, -1.0, diag=True, step=2)
+    ef_("sr", 0, 6, 10, -1.0, step=2); ef_("sr", 0, 7, 10, 1.0, step=2)
+    eb_("b", 14, 14, 16, 0.5, diag=True)
+    eb_("sg", 15, 2, 6, K, step=2); eb_("sg", 15, 3, 6, -K, step=2)
+    eb_("sg", 15, 6, 10, K, step=3); eb_("sg", 15, 7, 9, -K); eb_("win", 0, 10, 11, 1.0)
+    ef_("rt", 14, 4, 6, 1.0); ef_("rt", 15, 4, 6, 1.0)
+    ef_("h", 0, 0, 16, 0.5, diag=True); ef_("h", 12, 12, 14, 1.0, diag=True)
+    eb_("y", 0, 0, 12, 255 / 1024, diag=True); eb_("y", 15, 0, 12, -0.25); eb_("y", 15, 14, 16, -1 / 1024)
+    eb_("q", 0, 12, 14, 1.0); eb_("q", 1, 12, 14, BIG)
+    eb_("qs", 15, 12, 13, -K2); eb_("qs", 15, 13, 14, K2)
+    eb_("tot", 0, 0, 16, 1.0)
+
+    def ts(out, in0, s1, s2, o0, o1, r, w, el=1):
+        if o1 is None:
+            dve(lambda e: e.tensor_scalar(out, in0, s1, None, o0), r, w, el)
+        else:
+            dve(lambda e: e.tensor_scalar(out, in0, s1, s2, o0, o1), r, w, el)
+
+    def lin(out, in_, scale, bias, r, w, el=1, banks=(), f=F.Identity):
+        act(lambda e: e.activation(out, in_, f, bias=bias, scale=scale), r, w, el, banks)
+
+    ts(T.pmi[:, 1:2], T.pmi[:, 0:1], 15, None, A.bitwise_and, None, ["pmi0"], ["pmi1"])
+    dve(lambda e: e.tensor_copy(col("pm"), T.pmi[:, 1:2]), ["pmi1"], ["pm"], 1)
+    ts(T.oh[:], T.ki[:], col("pm"), None, A.is_equal, None, ["ki", "pm"], ["oh"])
+    dve(lambda e: e.tensor_tensor(T.oh2[:], T.oh[:, 0:16:2], T.oh[:, 1:16:2], A.add), ["oh"], ["oh2"], 16)
+    lin(col("cs"), col("pm"), -400.0, 5400.0, ["pm"], ["cs0"], f=F.Sigmoid)
+    ts(col("cs1"), col("cs"), 0.5, None, A.is_gt, None, ["cs0"], ["cs"])
+    lin(col("cb"), oh2(6), -2048.0, oh(15), ["oh", "oh2"], ["cb"])
+    dve(lambda e: e.tensor_copy(col("e"), T.sgi[:, 0:1]), ["sgi"], ["e"], 1)
+    lin(col("z"), oh(15), -0.5, col("e"), ["oh", "e"], ["z"])
+    g8 = T.bd[:, :, 0]
+    ts(T.wz[:, 0:8], g8, col("z"), -1.0, A.mult, A.mult, ["bd", "z"], ["wz0"])
+    ts(T.wz[:, 8:16], g8, col("z"), None, A.mult, None, ["bd", "z"], ["wz1"])
+    ts(T.wz[:, 16:24], g8, oh(12), None, A.mult, None, ["bd", "oh"], ["wz2"])
+    ts(T.wz[:, 24:32], g8, oh(13), None, A.mult, None, ["bd", "oh"], ["wz3"])
+    dve(lambda e: e.tensor_copy(T.ih[:], T.wf[:, 0]), ["wf_i"], ["ih"], 128)
+    for c in range(3):
+        dve(lambda e, c=c: e.tensor_copy(T["lz%d" % c][:], T.zero[:]), ["zero"], ["lz%d" % c], 136)
+    dve(lambda e: e.tensor_copy(T.wr1[:], T.zero[:, 0:128]), ["zero"], ["wr1"], 64)
+    ts(T.wr1[:, :, 14], g8, col("z"), -1.0, A.mult, A.mult, ["bd", "z", "wr1"], ["wr1"])
+    ts(T.wr1[:, :, 15], g8, col("z"), None, A.mult, None, ["bd", "z", "wr1"], ["wr1"])
+    lin(col("h14"), oh2(7), 0.5, 0.0, ["oh2"], ["h14"])
+    for i in range(1, 8):
+        lin(T.ident[:, i * idw:(i + 1) * idw], T.ident[:, 0:idw], 1.0, float(i * idw), ["id0"], ["id%d" % i], idw)
+    ids = ["id%d" % i for i in range(8)]
+    lin(T.dum[:], T.dum[:], 1.0, col("pm"), ["dum", "pm"], ["dum"], 24)
+    lin(T.wb[:, BFW.index("c"), :, 0:2], T.bd[:, :, 0:2], -1.0, 0.0, ["bd", "wb_c"], ["wb_c"], 16)
+    ts(col("ws0"), col("pm"), 10.5, 0.5, A.is_lt, A.mult, ["pm"], ["ws0"])
+    lin(col("ws"), oh(1), -0.5, col("ws0"), ["oh", "ws0"], ["ws"])
+    lin(wb["s"], T.bd[:], col("ws"), 0.0, ["bd", "ws", "wb_s"], ["wb_s"], 128)
+    lin(col("r0"), oh2(1), K - 3.5, 0.0, ["oh2"], ["r0"])
+    lin(col("r1"), oh2(2), K - 32.5, col("r0"), ["oh2", "r0"], ["r1"])
+    lin(col("r3"), oh(6), K - 0.5, col("r1"), ["oh", "r1"], ["r3"])
+    lin(col("r4"), oh(7), -K - 0.5, col("r3"), ["oh", "r3"], ["r4"])
+    lin(col("r5"), oh(8), K - 0.5, col("r4"), ["oh", "r4"], ["r5"])
+    lin(col("r2"), oh(9), -K - 0.5, col("r5"), ["oh", "r5"], ["r2"])
+    lin(col("hb"), oh2(7), -MAG, 0.0, ["oh2"], ["hb"])
+    lin(col("qb0"), oh2(6), V - BIG - K2, -1.0, ["oh2"], ["qb0"])
+    ts(col("os"), col("pm"), 11.5, 0.5, A.is_lt, A.mult, ["pm"], ["os"])
+    lin(col("ob"), col("os"), -256.0, 0.0, ["os"], ["ob"])
+    lin(col("d0"), oh(1), -1.0, 1.0, ["oh"], ["d0c"])
+    lin(T.d0[:], T.zero[:, 0:C], 1.0, col("d0"), ["zero", "d0c"], ["d0"], C)
+    lin(col("t0"), oh(0), -2.5 * 2.0 ** 97, 0.0, ["oh"], ["t0"])
+    dve(lambda e: e.tensor_tensor_scan(T.thr[:], T.half[:], T.zero[:, 0:C], col("t0"), A.mult, A.add), ["half", "zero", "t0"], ["thr"], 96)
+    ts(T.lt[:], T.ki[:], col("pm"), -0.5, A.is_lt, A.mult, ["ki", "pm"], ["lt"])
+    lin(T.lt[:], T.lt[:], 1.0, 1.0, ["lt"], ["lt"], 16)
+    dve(lambda e: e.tensor_tensor_scan(T.ww[:, 0:16], T.lt[:], T.zero[:, 0:16], 2.0 ** 96, A.mult, A.add), ["lt", "zero"], ["ww0"], 16)
+    dve(lambda e: e.tensor_tensor_scan(T.ww[:, 16:27], T.c16[:, 0:11], T.zero[:, 0:11], T.ww[:, 15:16], A.mult, A.add), ["c16", "zero", "ww0"], ["ww1"], 16)
+    ww = ["ww0", "ww1"]
+    dve(lambda e: e.tensor_copy(T.ix0[:], T.sti[:]), ["sti"], ["ix0"], 64)
+    for c, (o, m) in enumerate(CH):
+        lin(T.y0[:, o:o + m], T.cxb[:, o:o + m], 2.0, 256.0, ["cxb%d" % c], ["y0_%d" % c], m)
+    for i in range(LOADS):
+        dve(lambda e, i=i: e.tensor_copy(T.pool[:, BASE + lb_[i]:BASE + lb_[i + 1]], T.raw[:, lb_[i]:lb_[i + 1]]),
+            ["raw%d" % i], ["pool%d" % i], lb_[i + 1] - lb_[i])
+    allpool = ["poolA", "poolB"] + ["pool%d" % i for i in range(LOADS)]
+
+    def store0(v):
+        a, b = opt["store0"][v]
+        if b > a:
+            dma("sp", T.yp[:, a:b], T.pool[:, BASE + a:BASE + b], allpool + ["PW", "PC"], ["yp%d" % v], 512 * (b - a))
+
+    def bank(c, i):
+        return T["pb%d" % (2 * c + i)], "B%d" % (2 * c + i)
+
+    t0, t1 = T.pb6, T.pb7
+
+    def yin(v, c):
+        if v == 0:
+            return ["y0_%d" % c]
+        return ["y%d_%d" % (v, c)] + [["arr:y%d_a" % v], ["arr:y%d_1" % v, "arr:y%d_0" % v], ["arr:y%d_2" % v]][c]
+
+    def xpass(v, c, first, which):
+        o, m = CH[c]
+        p, b = bank(c, which)
+        k = ("x", "x2")[which]
+        pe([(p[:, 0:m], wb[k], T["y%d" % v][:, o:o + m], True, True, m)],
+           ["wb_" + k] + (yin(v, c) if first else ["y%d_%d" % (v, c)]), ["p%s%d" % (k, c)], [b])
+
+    def gather(v, c, k):
+        o, m = CH[c]
+        src = (T["ix%d" % v], T.i1, T.i2)[k]
+        if k > 0:
+            r = ["i%d_%d" % (k, c)]
+        elif v == 0:
+            r = ["ix0"]
+        else:
+            r = [["arr:i%d_1" % v], ["arr:i%d_1" % v, "arr:i%d_0" % v], ["arr:i%d_2" % v]][c]
+        act(lambda e: e.activation(T.rec[:, o:o + m], pw.indirect(src[:, o // 16:(o + m) // 16]), F.Identity, bias=col("cb"), scale=col("cs1")),
+            r + allpool + ["PW", "cb", "cs"], ["rec%d" % c], 60 + GA * m)
+        ops[-1]["lock"] = "r"
+
+    def step(v, c, k):
+        o, m = CH[c]
+        (p0, b0), (p1, b1) = bank(c, 0), bank(c, 1)
+        y = T["y%d" % v]
+        rc, pc, yc, xc, x2c = T.rec[:, o:o + m], T.pr[:, o:o + m], y[:, o:o + m], p0[:, 0:m], p1[:, 0:m]
+        dve(lambda e: e.tensor_tensor(pc, rc, xc, A.mult), ["rec%d" % c, "px%d" % c], ["pr%d" % c], m, [b0])
+        dve(lambda e: e.tensor_tensor(yc, rc, x2c, A.add), ["rec%d" % c, "px2%d" % c], ["y%d_%d" % (v, c)], m, [b1])
+        both = c > 0 and k in opt["merge"]
+        if both:
+            xpass(v, c, False, 1)
+            if c == 1:
+                return
+            xpass(v, c, False, 0)
+            c, o, m = 1, CH[1][0], S - C
+            (p0, b0), (p1, b1) = bank(c, 0), bank(c, 1)
+        M, a0, na = m // 8, o // 16, m // 16
+        lz, mk = T["lz%d" % c], T["mk%d" % c]
+        pe([(p0[0:M, q:256:8], T.pr[:, o + q:o + m:8], T.wz[:], True, True, max(min(M, 64), 32)) for q in range(8)],
+           ["pr%d" % c, "wz0", "wz1", "wz2", "wz3"] + (["pr2"] if both else []), ["px%d" % c], [b0])
+        if k < 2 and not both:
+            xpass(v, c, False, 1)
+        lin(mk[0:M, :], p0[0:M, 0:128], 400.0, 0.0, ["px%d" % c], ["mk%d" % c], 128, [b0], f=F.Sigmoid)
+        dve(lambda e: e.tensor_tensor(lz[0:M, 1:32:2, :], mk[0:M, :], p0[0:M, 128:256], A.mult), ["mk%d" % c, "px%d" % c], ["lz%d" % c], 128, [b0])
+        lo = p1[:, 416:416 + na]
+        pe([(lo, lz[0:M, 16 * (q // 2) + 1 - q % 2:16 * (q // 2) + 17 - q % 2, :], T.ih[0:M, q % 2:M:2], q == 0, q == 3, 64) for q in range(4)],
+           ["lz%d" % c, "ih"], ["lo%d" % c], [b1])
+        if k < 2:
+            xpass(v, c, False, 0)
+        if k == 2 and v == 2 and c > 0:
+            lin(T.fs[:, a0:a0 + na], lo, 1.0, 2048.0, ["lo%d" % c], ["fs%d" % c], na, [b1])
+        else:
+            dst = (T.i1, T.i2, T["io%d" % v])[k]
+            nm = "i%d_%d" % (k + 1, c) if k < 2 else "io%d_%d" % (v, c)
+            dve(lambda e: e.tensor_scalar(dst[:, a0:a0 + na], lo, 2048.0, None, A.add), ["lo%d" % c], [nm] + (["i%d_2" % (k + 1)] if both else []), na, [b1])
+        if c == 0 and k == 1:
+            lin(T.sf[:], lo, 1.0, 2048.0, ["lo0"], ["sf"], 12, [b1])
+            lin(T.el1[:], lo, 1.0, 2048.0 + BASE - 1 - BIG, ["lo0"], ["el1"], 12, [b1])
+        if c == 0 and k == 2:
+            lin(T.tf[:], lo, 1.0, 2048.0, ["lo0"], ["tf"], 12, [b1])
+            lin(T.el2[:, 12:24], lo, 1.0, 2048.0 + BASE - 1 - BIG, ["lo0"], ["el2b"], 12, [b1])
+            lin(T.tb[:], lo, 1.0, 2048.0 + BASE, ["lo0"], ["tb"], 12, [b1])
+        if k == 2:
+            no = (416, 0, 608)[c]
+            if v < 2:
+                if c == 1:
+                    send(1, T["y%d" % (v + 1)][:, 0:C], y[:, o:o + C], ["y%d_1" % v], "y%d_a" % (v + 1), 256 * C)
+                    send(1, T["y%d" % (v + 1)][:, C:m], y[:, o + C:o + m], ["y%d_1" % v], "y%d_1" % (v + 1), 256 * m)
+                else:
+                    send(1, T["y%d" % (v + 1)][:, no:no + m], y[:, o:o + m], ["y%d_%d" % (v, c)], "y%d_%d" % (v + 1, c), 256 * m)
+                if c > 0:
+                    send(1, T["ix%d" % (v + 1)][:, no // 16:no // 16 + na], T["io%d" % v][:, a0:a0 + na], ["io%d_%d" % (v, c)], "i%d_%d" % (v + 1, c), 256 * na)
+            else:
+                lin(T.xo[:, o:o + m], y[:, o:o + m], col("os"), col("ob"), ["y2_%d" % c, "os", "ob"], ["xo%d" % c], m)
+                send(-2, T.xland[:, o:o + m], T.xo[:, o:o + m], ["xo%d" % c], "xf%d" % c, 256 * m)
+                for j, p, m1 in [[(384, 0, 192)], [(576, 192, 32), (0, 224, 384)], [(608, 608, 416)]][c]:
+                    dma("sp", T.yx[:, j:j + m1], T.xland[:, p:p + m1], ["arr:xf%d" % c], [], 256 * m1)
+                if c == 2:
+                    send(-2, T.fland[:, 12:64], T.fs[:, 12:64], ["fs1", "fs2"], "ff", 512 * 52)
+                    for j, p, m1 in [(36, 12, 2), (0, 14, 24), (38, 38, 26)]:
+                        dma("sp", T.ys[:, j:j + m1], T.fland[:, p:p + m1], ["arr:ff"], [], 512 * m1)
+
+    def pick(out, win, idx, r, w):
+        act(lambda e: e.activation(out, win.indirect(idx), F.Identity), r, w, 60 + GA * C)
+
+    def compare(row, rown, lst, lstn, wt, wtn, out, b, outn, close):
+        for a in range(12):
+            ts(T.eb[:, a, 16 * a:C], row[:, 16 * a:C], lst[:, a:a + 1], wt[:, a:a + 1], A.is_equal, A.mult,
+               [rown, lstn] + wtn, ["eb%d" % a], C - 16 * a)
+        for x in (range(0, 6), range(6, 12)):
+            pe([(out[:, 16 * u:C], wb["c"], T.eb[:, u, 16 * u:C], False, close and u == 11, max(64, C - 16 * u)) for u in x],
+               ["eb%d" % u for u in x] + ["wb_c", outn], [outn], [b])
+
+    def tolist(out, early, rhs):
+        return [(out, wf["i"], early, True, False, 256)] + [(out, T.wl[:, 15 - r:143 - r], rhs(r), False, r == 15, 64) for r in range(16)]
+
+    def early(v):
+        s = T.i2[:, 0:12]
+        pick(T.srow[:], T.ident[:, 0:W], s, ["i2_0"] + ids, ["srow"])
+        pick(T.recs_[:], pw, s, ["i2_0", "PW", "PC"] + allpool, ["recs"])
+        pe([(t0[:, 0:C], wb["c"], T.thr[:], True, False, C)], ["wb_c", "thr"], ["r0p"], ["B6"])
+        compare(T.srow, "srow", T.sf, "sf", T.ww[:, 15:27], ww, t0, "B6", "r0p", True)
+        lin(T.sg1[:], t0[:, 0:C], 1.0, 0.0, ["r0p"], ["sg1"], C, ["B6"], f=F.Sign)
+        pe(tolist(t0[:, 192:204], T.el1[:], lambda r: T.sg1[:, r:C:16]), ["wf_i", "el1", "wl", "sg1"], ["p1"], ["B6"])
+        dve(lambda e: e.tensor_tensor(T.s1f[:], t0[:, 192:204], T.dum[:, 12:24], A.max), ["p1", "dum"], ["s1f"], 12, ["B6"])
+        dve(lambda e: e.tensor_copy(T.si[:, 0:12], T.s1f[:]), ["s1f"], ["si0"], 12)
+        lin(T.wbig[:], t0[:, 192:204], 1e29, 0.0, ["p1"], ["wbig"], 12, ["B6"], f=F.Relu)
+        dve(lambda e: e.tensor_tensor(T.w1[:], T.wbig[:], T.ww[:, 15:27], A.min), ["wbig"] + ww, ["w1"], 24)
+        lin(T.el2[:, 0:12], T.dum[:, 0:12], 0.0, col("lb%d" % v), ["dum", "lb%d" % v], ["el2a"], 12)
+
+    def stage1(v):
+        r1, bs = t1[:, 256:448], t0[:, 256:448]
+        pe([(r1, T.wr1[:], T.pr[:, 0:C], True, True, C)], ["wr1", "pr0"], ["r1p"], ["B7"])
+        dve(lambda e: e.tensor_scalar(T.inc[:], r1, 0.0, None, A.is_gt), ["r1p"], ["inc"], C, ["B7"])
+        lin(T.sgn[:], r1, 1.0, 0.0, ["r1p"], ["sgn"], C, ["B7"], f=F.Sign)
+        pe([(t1[:, 0:C], wb["c"], T.thr[:], True, False, C), (t1[:, 0:C], wb["win"], T.sg1[:], False, False, C),
+            (t1[:, 0:C], wb["sg"], T.sgn[:], False, False, C)], ["wb_c", "thr", "wb_win", "sg1", "wb_sg", "sgn"], ["r2p"], ["B7"])
+        pe([(t1[:, 0:C], wf["sr"], T.srow[:], False, False, 4 * C)], ["wf_sr", "srow", "r2p"], ["r2p"], ["B7"])
+        pe([(t1[:, 0:C], wf["rs"], T.recs_[:], False, False, 4 * C)], ["wf_rs", "recs", "r2p"], ["r2p"], ["B7"])
+        pe([(bs, wf["i"], T.recs_[:], True, False, 4 * C), (bs, wb["b"], T.sgn[:], False, True, C)], ["wf_i", "recs", "wb_b", "sgn"], ["bsp"], ["B6"])
+        lin(T.bn[:, 0:C], bs, 1.0, col("h14"), ["bsp", "h14"], ["bn0"], C, ["B6"])
+
+    def scat1(v):
+        dve(lambda e: e.tensor_tensor(pall.indirect(T.si[:, 0:12]), T.recs_[:], T.inc[:], A.add), ["si0", "recs", "inc"], ["PC"], 60 + SC * C)
+        ops[-1]["lock"] = "w"
+        pick(T.bn[:, 2 * C:], pw, T["io%d" % v][:, 0:12], ["io%d_0" % v, "PW", "PC"], ["rect"])
+        if v == 2:
+            for i in (14, 15):
+                dma("sp", T.cnt2[i:128:16, BASE:], T.pool[i:128:16, BASE:], ["PW", "PC"], ["cnt%d" % i], 120000 * (i - 13))
+
+    def late(v):
+        t = T["io%d" % v][:, 0:12]
+        (a0, ba0), (a1, ba1) = bank(0, 0), bank(0, 1)
+        pick(T.trow[:], T.ident[:, 0:W], t, ["io%d_0" % v] + ids, ["trow"])
+        compare(T.trow, "trow", T.tf, "tf", T.w1, ["w1"], t1, "B7", "r2p", False)
+        pe([(t1[:, 0:C], wf["rt"], T.bn[:, 2 * C:], False, True, 4 * C)], ["wf_rt", "rect", "r2p"], ["r2p"], ["B7"])
+        r3 = a1[:, 192:384]
+        pe([(r3, wb["y"], T["y%d" % v][:, 0:C], True, False, C), (r3, wf["h"], T.bn[:, 2 * C:], False, True, 4 * C)],
+           ["wb_y", "wf_h", "rect", "y%d_0" % v], ["r3p"], [ba1])
+        lin(T.rr[:], r3, 1.0, MAG, ["r3p"], ["rr"], C, [ba1])
+        lin(T.bn[:, C:2 * C], T.rr[:], 1.0, -MAG, ["rr"], ["bn1"], C)
+        lin(T.hz[:, C:], T.rr[:], oh2(7), col("hb"), ["rr", "oh2", "hb"], ["hm"], C)
+        lin(T.fl[:], t1[:, 0:C], 1.0, col("r2"), ["r2p", "r2"], ["fl"], C, ["B7"], f=F.Sign)
+        pe([(t0[:, 0:C], wb["s"], T.fl[:], True, True, C)], ["wb_s", "fl"], ["r0p"], ["B6"])
+        lin(T.cr[:, 1], t0[:, 0:C], 1.0, -2.0, ["r0p"], ["cr1"], C, ["B6"], f=F.Relu)
+        dve(lambda e: e.tensor_tensor_scan(T.cr[:, 0], T.d0[:], T.cr[:, 1], 0.0, A.mult, A.add), ["d0", "cr1"], ["cr0"], 96)
+        pe([(a0[:, 0:C], wb["qs"], T.sgn[:], True, False, C)], ["wb_qs", "sgn"], ["px0"], [ba0])
+        pe([(a0[:, 0:C], wb["q"], T.cr[:, 0], False, True, C)], ["wb_q", "cr0", "px0"], ["px0"], [ba0])
+        pe(tolist(t0[:, 204:228], T.el2[:], lambda r: T.cr[:, :, r:C:16]), ["wf_i", "el2a", "el2b", "wl", "cr0", "cr1"], ["p2"], ["B6"])
+        lin(T.qn[:, 0:C], a0[:, 0:C], 1.0, col("qb%d" % v), ["px0", "qb%d" % v], ["qn0"], C, [ba0])
+        dve(lambda e: e.tensor_tensor(T.idf[:], t0[:, 204:228], T.dum[:], A.max), ["p2", "dum"], ["idf"], 24, ["B6"])
+        dve(lambda e: e.tensor_copy(T.si[:, 12:36], T.idf[:]), ["idf"], ["si1"], 24)
+        dve(lambda e: e.tensor_tensor(T.ncf[:], T.idf[:, 0:12], T.tb[:], A.max), ["idf", "tb"], ["ncf"], 24)
+        if v < 2:
+            ts(T["nc%d" % v][:], T.ncf[:], -float(BASE), None, A.add, None, ["ncf"], ["nc%d" % v], 12)
+            send(1, T["ix%d" % (v + 1)][:, 26:38], T["nc%d" % v][:], ["nc%d" % v], "i%d_0" % (v + 1), 256 * 12)
+            pe([(t1[:, 256:257], wb["tot"], T.cr[:, 0, C - 1:C], True, True, 64)], ["wb_tot", "cr0"], ["totp"], ["B7"])
+            lin(col("qb%d" % (v + 1)), t1[:, 256:257], oh2(6), col("qb%d" % v), ["totp", "oh2", "qb%d" % v], ["qb%d" % (v + 1)], 1, ["B7"])
+            lin(col("lb%d" % (v + 1)), t1[:, 256:257], 1.0, col("lb%d" % v), ["totp", "lb%d" % v], ["lb%d" % (v + 1)], 1, ["B7"])
+        else:
+            lin(T.fs[:, 0:12], T.ncf[:], 1.0, -float(BASE), ["ncf"], ["fs0"], 12)
+            send(-2, T.fland[:, 0:12], T.fs[:, 0:12], ["fs0"], "f0", 512 * 12)
+            dma("sp", T.ys[:, 24:36], T.fland[:, 0:12], ["arr:f0"], [], 512 * 12)
+        dve(lambda e: e.tensor_tensor(pall.indirect(T.si[:, 0:24]), T.bn[:, 0:2 * C], T.qn[:], A.max),
+            ["si0", "si1", "bn0", "bn1", "qn0", "qn1"], ["PW", "PC"], 60 + SC * 2 * C)
+
+    def scat_t():
+        pick(T.g2[:], pall, T.si[:, 24:36], ["si1", "PW", "PC"], ["g2"])
+        dve(lambda e: e.tensor_tensor(pall.indirect(T.si[:, 24:36]), T.g2[:], T.hz[:, C:], A.subtract),
+            ["si1", "g2", "hm"], ["PC"], 60 + SC * C)
+        ops[-1]["lock"] = "w"
+
+    for v in range(3):
+        if v == 0:
+            store0(0)
+        for c in range(3):
+            xpass(v, c, True, 0)
+            xpass(v, c, True, 1)
+        gather(v, 0, 0); step(v, 0, 0)
+        if v > 0:
+            scat_t()
+            store0(v)
+        gather(v, 0, 1); step(v, 0, 1)
+        early(v)
+        gather(v, 0, 2); step(v, 0, 2)
+        stage1(v)
+        for k in range(3):
+            for c in (1, 2):
+                gather(v, c, k); step(v, c, k)
+        scat1(v)
+        late(v)
+    dve(lambda e: e.tensor_tensor(T.cnt2[:, 0:BASE + W].indirect(T.si[:, 12:36]), T.bn[:, C:], T.hz[:], A.subtract),
+        ["si1", "bn1", "rect", "hm", "hz0", "cnt14", "cnt15"], ["cnt"], 60 + SC * 2 * C)
+    yps = ["yp0", "yp1", "yp2"]
+    for i in range(8):
+        dma("act" if i % 2 else "sp", T.yp[16 * i:16 * i + 12, V:W], T.pool[16 * i:16 * i + 12, BASE + V:], ["PW", "PC"], [], 30000 * (i + 1))
+    for i in (12, 13):
+        dma("sp", T.yp[i:128:16, :], T.pool[i:128:16, BASE:], ["PW", "PC"] + yps, [], 240000 + 120000 * (i - 11))
+    for i in (14, 15):
+        dma("sp" if i == 14 else "act", T.yp[i:128:16, :], T.cnt2[i:128:16, BASE:], ["cnt"] + yps, [], 200000 + 120000 * (i - 13))
+    return ops
+
+
+def edges(ops):
+    lastw, readers, bk, deps = {}, {}, {}, []
+    for i, o in enumerate(ops):
+        d = {}
+        for x in o["r"]:
+            if x in lastw:
+                d[lastw[x]] = True
+        for x in o["w"]:
+            for j in ([lastw[x]] if x in lastw else []) + readers.get(x, []):
+                d[j] = True
+        for b in o["banks"]:
+            for e2, j in bk.setdefault(b, {}).items():
+                d[j] = d.get(j, False) or e2 != o["eng"]
+            bk[b][o["eng"]] = i
+        for j in list(d):
+            if ops[j]["eng"] == "pe" and o["eng"] == "pe":
+                d[j] = False
+        d.pop(i, None)
+        deps.append(d)
+        for x in o["r"]:
+            readers.setdefault(x, []).append(i)
+        for x in o["w"]:
+            lastw[x] = i
+            readers[x] = []
+    return deps
+
+
+def waits(ops, deps, order):
+    pos, cnt = {}, {}
+    for i in order:
+        if ops[i]["kind"] == "c":
+            cnt[ops[i]["eng"]] = cnt.get(ops[i]["eng"], 0) + 1
+            pos[i] = cnt[ops[i]["eng"]]
+    rank = {i: k for k, i in enumerate(order)}
+    known, clock, need = {}, {}, {}
+    for i in order:
+        kn = known.setdefault(ops[i]["eng"], {})
+        need[i] = []
+        for j in sorted([j for j in deps[i] if deps[i][j]], key=lambda j: -rank[j]):
+            key, val = (ops[j]["eng"], pos[j]) if ops[j]["kind"] == "c" else (ops[j]["sem"], 1)
+            if kn.get(key, 0) >= val:
+                continue
+            need[i].append(j)
+            for k2, v2 in clock[j].items():
+                kn[k2] = max(kn.get(k2, 0), v2)
+        if ops[i]["kind"] == "c":
+            clock[i] = dict(kn); clock[i][ops[i]["eng"]] = pos[i]
+        elif ops[i]["kind"] == "dma":
+            clock[i] = dict(kn); clock[i][ops[i]["sem"]] = 1
+        else:
+            clock[i] = {ops[i]["sem"]: 1}
+    return need
+
+
+OPT = {"par": (1.0, 0.5, 1.56, 3.8, 2500), "loads": [0, 896, 1792, 2688, 3072], "store0": [(0, 2048), (2048, 3072), (0, 0)], "merge": [0, 1],
+       "order": "05060h0x0304070100020i0n0e2a0g0y230m0a0b2e0q2c22171w1c342d1p181q191r2b1s1a30240f1b1v092f080k0o0l260c2g0p3135320r331t1x382i0s2h2y4s2s2w0t2x0u2m1u3d2n201y211z2t0v2z29272o28472p0d0w2j0j2k252l0z2u3e102q2r39152v161f1d111e1k1l1g3a1213141m3b1h1i3c3j5h1j3l3k1n3n1o3m373o3h363p3q5i5d3f3s3r3i3t3g5e3u5m3v5f3w5n3x3y5o5g3z5j4041425p5q455r5l43445k4t4b4c485s4a4u4j4i4w4d495w554h4e4k4g4f5t4x4l465x4m4v6156545u4n57624y635v4o4p4z4q4r58506s5b6u5152595c6x6v6t656y6z64536w5a706671756777737274765y78796i6860696a7e7a6j6b6g6c7f6f7b6l7g6d6m7i6e5z7c7h6n6h7d7k6k6q7j7m6o7l7r7o7n8s7p7s7u7t7q9d6p7v816r7w8b7y827x838c848586879y8d88898a7z8ea0808fa2a18g8h9z8i8j8ka38l8m8na4a78o8qa5a88y8ra6a98z8xaa8p9e8uab8vac8tad8w90929594919g93ah9f9p96ae9q9h9r97ai9s989iaj9jam999a9kanaf9t9b9l9wao9m9cbd9n9obfagap9xaqbhbec3bi9uarbjasblbp9vbrbobgbqbkalbnb3bmbsataubtavb4b1buawb0axb6bzayb7c0azakb8c1b2bvc2b5c5bwbbbxbyc4c7b9c6dcc9c8bacccacfcbcdcedxbccgchcmcicjcwcncocpcxcqcrcsekctcucvckclcyeleoczd0d1emd2d3d4enepd5d6d7eqetdad8eseudedyerevddd9ewdbdfexdzdge1dhdieceye2dldpdjezdndmdodkeddqe3e0drf1e4eedse9f0f3eae5f2dtefdug9f4egdve6g5e7e8f8gxf9eifag6g7dwg8f5fbfcejfdgff6gefegaehgdgbf7gcfqgggmghgjglgiebgkfggnffgofmfrfhgtfngufsfiftgvfjgpfygwfugyfzgzh0fvgqgrfkh1fwflh2h3fxh7h4gsg1h5h8hbhahdhehihch9hghhhffofphjhkg4g3g0g2h6"}
+
+
+def rank_program(g, core, T, topo):
+    if T.rank_of(core) is None:
+        return
+    ops = build(T, topo, core, OPT)
+    deps = edges(ops)
+    order = [int(OPT["order"][i:i + 2], 36) for i in range(0, len(OPT["order"]), 2)]
+    seen = {"r": [], "w": []}
+    for i in order:
+        k = ops[i]["lock"]
+        if k:
+            for j in seen["w" if k == "r" else "r"]:
+                deps[i][j] = True
+            seen[k].append(i)
+    need = waits(ops, deps, order)
+    q = {"pe": g.tensor, "act": g.scalar, "dve": g.vector, "g": g, "sp": g.sync}
+    marked = set(j for i in order for j in need[i])
+    val, cnt, sent = {}, {}, 0
+    for i in order:
+        o = ops[i]
+        e = q[o["eng"]]
+        for j in need[i]:
+            if ops[j]["kind"] == "c":
+                e.wait_ge(T.sem["c_" + ops[j]["eng"]], val[j])
+            else:
+                e.wait_ge(T.sem[ops[j]["sem"]], ops[j]["inc"])
+        ins = o["fn"](e)
+        if o["kind"] == "c":
+            if i in marked:
+                cnt[o["eng"]] = cnt.get(o["eng"], 0) + 1
+                val[i] = cnt[o["eng"]]
+                ins.then_inc(T.sem["c_" + o["eng"]], 1)
+        elif o["kind"] == "dma":
+            ins.then_inc(T.sem[o["sem"]], 16)
+        else:
+            sent += o["loc"]
+    g.wait_ge(T.sem.sent, sent)
+    for i in order:
+        if ops[i]["kind"] == "dma" and i not in marked:
+            g.sync.wait_ge(T.sem[ops[i]["sem"]], 16)

@@ -4,87 +4,62 @@ V, S, C, W = 3072, 1024, 192, 3648
 BASE = 384
 K, BIG, K2, MAG = 8192.0, 4096.0, 2048.0, 12582912.0
 CH = [(0, 192), (192, 416), (608, 416)]
-BFW = ["x", "x2", "y", "b", "sg", "win", "c", "s", "q", "qs", "tot"]
+BFW = ["x", "x2", "y", "sg", "win", "c", "s", "q", "qs", "tot"]
 F32W = ["i", "rs", "sr", "rt", "h"]
 
-SCRATCH = {
-    "raw": ("sbuf", [128, V], "int32"), "pool": ("sbuf", [128, BASE + W], "float32"),
-    "cnt2": ("sbuf", [128, BASE + W], "float32"), "ident": ("sbuf", [128, W], "float32"),
-    "sgi": ("sbuf", [128, 4], "int32"), "sti": ("sbuf", [128, 64], "int32"), "cxb": ("sbuf", [128, S], "bfloat16"),
-    "rec": ("sbuf", [128, S], "float32"), "pr": ("sbuf", [128, S], "float16"),
-    "wb": ("sbuf", [128, len(BFW), 8, 16], "bfloat16"), "wf": ("sbuf", [128, len(F32W), 8, 16], "float32"),
-    "wl": ("sbuf", [128, 144], "bfloat16"), "wz": ("sbuf", [128, 32], "float16"), "wr1": ("sbuf", [128, 8, 16], "float16"),
-    "ih": ("sbuf", [128, 128], "float16"), "bd": ("sbuf", [128, 8, 16], "bfloat16"),
-    "zero": ("sbuf", [128, 272], "bfloat16"), "half": ("sbuf", [128, C], "bfloat16"), "c16": ("sbuf", [128, 16], "float32"),
-    "pmi": ("sbuf", [128, 2], "int32"), "ki": ("sbuf", [128, 16], "float32"), "oh": ("sbuf", [128, 16], "float32"),
-    "oh2": ("sbuf", [128, 8], "float32"), "lt": ("sbuf", [128, 16], "float32"), "ww": ("sbuf", [128, 28], "float32"),
-    "col": ("sbuf", [128, 40], "float32"), "dum": ("sbuf", [128, 24], "float32"),
-    "thr": ("sbuf", [128, C], "bfloat16"), "d0": ("sbuf", [128, C], "bfloat16"),
-    "i1": ("sbuf", [128, 64], "uint16"), "i2": ("sbuf", [128, 64], "uint16"),
-    "sf": ("sbuf", [128, 12], "float32"), "tf": ("sbuf", [128, 12], "float32"), "tb": ("sbuf", [128, 12], "float32"),
-    "el1": ("sbuf", [128, 12], "float32"), "el2": ("sbuf", [128, 24], "float32"),
-    "srow": ("sbuf", [128, C], "float32"), "trow": ("sbuf", [128, C], "float32"),
-    "recs_": ("sbuf", [128, C], "float32"), "g2": ("sbuf", [128, C], "float32"),
-    "eb": ("sbuf", [128, 12, C], "bfloat16"), "sg1": ("sbuf", [128, C], "bfloat16"), "sgn": ("sbuf", [128, C], "bfloat16"),
-    "fl": ("sbuf", [128, C], "bfloat16"), "cr": ("sbuf", [128, 2, C], "bfloat16"),
-    "s1f": ("sbuf", [128, 12], "float32"), "wbig": ("sbuf", [128, 12], "float32"), "w1": ("sbuf", [128, 12], "float32"),
-    "si": ("sbuf", [128, 36], "uint16"), "idf": ("sbuf", [128, 24], "float32"), "ncf": ("sbuf", [128, 12], "float32"),
-    "bn": ("sbuf", [128, 3 * C], "float32"), "qn": ("sbuf", [128, 2 * C], "float32"), "hz": ("sbuf", [128, 2 * C], "float32"),
-    "inc": ("sbuf", [128, C], "float32"), "rr": ("sbuf", [128, C], "float32"),
-    "fs": ("sbuf", [128, 64], "float32"), "fland": ("sbuf", [128, 64], "float32"),
-    "xo": ("sbuf", [128, S], "bfloat16"), "xland": ("sbuf", [128, S], "bfloat16"),
-}
-for _v in range(3):
-    SCRATCH["y%d" % _v] = ("sbuf", [128, S], "bfloat16")
-    SCRATCH["ix%d" % _v] = ("sbuf", [128, 64], "uint16")
-    SCRATCH["io%d" % _v] = ("sbuf", [128, 64], "uint16")
-    SCRATCH["nc%d" % _v] = ("sbuf", [128, 12], "uint16")
-    SCRATCH["lz%d" % _v] = ("sbuf", [128, 34, 8], "float16")
-    SCRATCH["mk%d" % _v] = ("sbuf", [128, 128], "bfloat16")
+SCRATCH = {}
+for _d, _l in {
+    "int32": [("raw", [V]), ("sgi", [4]), ("sti", [64]), ("pmi", [2])],
+    "float32": [("pool", [BASE + W]), ("cnt2", [BASE + W]), ("ident", [W]), ("rec", [S]), ("wf", [5, 8, 16]), ("c16", [16]), ("ki", [16]),
+                ("oh", [16]), ("oh2", [8]), ("lt", [16]), ("ww", [28]), ("col", [40]), ("dum", [24]), ("sf", [12]), ("tf", [12]), ("tb", [12]),
+                ("el1", [12]), ("el2", [24]), ("recs_", [C]), ("g2", [C]), ("s1f", [12]), ("wbig", [12]), ("w1", [12]), ("idf", [24]),
+                ("ncf", [12]), ("bn", [3 * C]), ("qn", [2 * C]), ("hz", [2 * C]), ("inc", [C]), ("rr", [C]), ("fs", [64]), ("fland", [64])],
+    "bfloat16": [("cxb", [S]), ("wb", [10, 8, 16]), ("wl", [144]), ("bd", [8, 16]), ("zero", [272]), ("half", [C]), ("thr", [C]), ("d0", [C]),
+                 ("eb", [12, C]), ("sg1", [C]), ("sgn", [C]), ("fl", [C]), ("cr", [2, C]), ("xo", [S]), ("xland", [S]),
+                 ("y0", [S]), ("y1", [S]), ("y2", [S]), ("mk0", [128]), ("mk1", [128]), ("mk2", [128])],
+    "float16": [("pr", [S]), ("wz", [32]), ("wr1", [8, 16]), ("ih", [128]), ("srow", [C]), ("trow", [C]), ("wsr", [8, 16]),
+                ("lz0", [34, 8]), ("lz1", [34, 8]), ("lz2", [34, 8])],
+    "uint16": [("i1", [64]), ("i2", [64]), ("si", [36]), ("ix0", [64]), ("ix1", [64]), ("ix2", [64]), ("io0", [64]), ("io1", [64]),
+               ("io2", [64]), ("nc0", [12]), ("nc1", [12])],
+}.items():
+    for _n, _s in _l:
+        SCRATCH[_n] = ("sbuf", [128] + _s, _d)
 for _b in range(8):
     SCRATCH["pb%d" % _b] = ("psum", [128, 512], "float32")
-
-N_DMA, N_ARR = 36, 20
-SEMAPHORES = (["c_pe", "c_act", "c_dve", "c_g", "sent"] + ["d%d" % i for i in range(N_DMA)]
-              + ["a%d" % i for i in range(N_ARR)])
-HOP = 120.0
+SEMAPHORES = ["c_pe", "c_act", "c_dve", "c_g", "sent"] + ["d%d" % i for i in range(36)] + ["a%d" % i for i in range(20)]
 
 
-def build(T, topo, core, opt):
+def build(T, topo, core):
     ops = []
-    CY, PCY, GA, SC, RL = opt["par"]
     n = len(T.cores)
     rank = T.rank_of(core)
     cnt = {"d": 0, "a": 0}
 
-    def op(eng, fn, r, w, cost, banks=(), kind="c", lat=0.0, sem=None, inc=0):
-        ops.append(dict(eng=eng, fn=fn, r=list(r), w=list(w), cost=cost, banks=list(banks), kind=kind, lat=lat, sem=sem, inc=inc, lock=None))
+    def op(eng, fn, r, w, banks=(), kind="c", sem=None, inc=0):
+        ops.append(dict(eng=eng, fn=fn, r=list(r), w=list(w), banks=list(banks), kind=kind, sem=sem, inc=inc, lock=None))
 
-    def dve(fn, r, w, el, banks=()):
-        op("dve", fn, r, w, max(64, el) * CY, banks)
-
-    def act(fn, r, w, el, banks=()):
-        op("act", fn, r, w, max(64, el) * CY + 20, banks)
+    def dve(fn, r, w, banks=()):
+        op("dve", fn, r, w, banks)
 
     def pe(mms, r, w, banks):
         def fn(e):
             last = None
             for m in mms:
-                last = e.matmul(m[0], m[1], m[2], m[3], m[4])
+                last = e.matmul(*m)
             return last
-        op("pe", fn, r, w, sum(m[5] for m in mms) * PCY + 40, banks)
+        op("pe", fn, r, w, banks)
 
-    def dma(q, out, in_, r, w, nbytes):
+    def dma(q, out, in_, r, w):
         sem = "d%d" % cnt["d"]; cnt["d"] += 1
-        op(q, lambda e: e.dma_start(out, in_), r, w, 60, kind="dma", lat=2000 + nbytes / 200.0, sem=sem, inc=16)
+        op(q, lambda e: e.dma_start(out, in_), r, w, kind="dma", sem=sem, inc=16)
 
-    def send(step, out, in_, r, name, nbytes):
+    def send(step, out, in_, r, name):
         dst, src = T.cores[(rank + step) % n], T.cores[(rank - step) % n]
         sem = "a%d" % cnt["a"]; cnt["a"] += 1
         rid, pid, _ = topo.addr(dst)
         m = topo.mask(core, dst)
-        op("g", lambda e: e.remote_dma(out, in_, T.sem[sem], T.sem.sent, pid, rid, m), r, ["arr:" + name], 400,
-           kind="rem", lat=RL + nbytes / 60.0, sem=sem, inc=len(topo.engines(src, core)))
+        op("g", lambda e: e.remote_dma(out, in_, T.sem[sem], T.sem.sent, pid, rid, m), r, ["arr:" + name],
+           kind="rem", sem=sem, inc=len(topo.engines(src, core)))
         ops[-1]["loc"] = len(topo.engines(core, dst))
 
     wb = {k: T.wb[:, i] for i, k in enumerate(BFW)}
@@ -102,45 +77,54 @@ def build(T, topo, core, opt):
     def oh2(i):
         return T.oh2[:, i:i + 1]
 
+    def fill(ap, c, w):
+        dve(lambda e: e.memset(ap, c), [], w)
+
+    def cp(out, in_, r, w):
+        dve(lambda e: e.tensor_copy(out, in_), r, w)
+
+    def tt(out, a, b, o, r, w, banks=()):
+        dve(lambda e: e.tensor_tensor(out, a, b, o), r, w, banks)
+
+    def ts(out, in0, s1, s2, o0, o1, r, w, banks=()):
+        if o1 is None:
+            dve(lambda e: e.tensor_scalar(out, in0, s1, None, o0), r, w, banks)
+        else:
+            dve(lambda e: e.tensor_scalar(out, in0, s1, s2, o0, o1), r, w, banks)
+
+    def scan(out, a, b, ini, r, w):
+        dve(lambda e: e.tensor_tensor_scan(out, a, b, ini, A.mult, A.add), r, w)
+
+    def lin(out, in_, scale, bias, r, w, banks=(), f=F.Identity):
+        op("act", lambda e: e.activation(out, in_, f, bias=bias, scale=scale), r, w, banks)
+
+    def iota(out, pat, base, w):
+        op("g", lambda e: e.iota(out, pat, base, 0, allow_small_or_imprecise_dtypes=True), [], w)
+
+    def sel(ap, pat, o, val, base, cm, nm):
+        op("g", lambda e: e.affine_select(ap, ap, pat, o, float(val), base, cm), [nm], [nm])
+
     pw = T.pool[:, BASE:BASE + W]
     pall = T.pool[:, 0:BASE + W]
-
-    lb_ = opt["loads"]
-    LOADS = len(lb_) - 1
-    dma("sp", T.sgi[:, 0:1], T.sg[:], [], ["sgi"], 512)
-    dma("act", T.sti[:], T.st0[:], [], ["sti"], 32768)
-    dma("act", T.cxb[:, 0:C], T.cx0[:, 0:C], [], ["cxb0"], 80000)
-    for i in range(LOADS):
-        dma("sp" if i % 2 == 0 else "act", T.raw[:, lb_[i]:lb_[i + 1]], T.recs[:, lb_[i]:lb_[i + 1]], [], ["raw%d" % i], 80000 + 512 * lb_[i + 1])
-    dma("sp", T.cxb[:, C:], T.cx0[:, C:], [], ["cxb1", "cxb2"], 1860000)
-    dve(lambda e: e.memset(T.bd[:], 1.0), [], ["bd"], 64)
-    dve(lambda e: e.memset(T.wb[:, 0:2], 0.0), [], ["wb_x", "wb_x2"], 128)
-    dve(lambda e: e.memset(T.wf[:, 0:1], 0.0), [], ["wf_i"], 128)
-    dve(lambda e: e.memset(T.wb[:, 2:], 0.0), [], ["wb_" + k for k in BFW[2:]], 64 * 9)
-    dve(lambda e: e.memset(T.wf[:, 1:], 0.0), [], ["wf_" + k for k in F32W[1:]], 128 * 5)
-    dve(lambda e: e.memset(T.wl[:], 0.0), [], ["wl"], 72)
-    dve(lambda e: e.memset(T.zero[:], 0.0), [], ["zero"], 136)
-    dve(lambda e: e.memset(T.half[:], 0.5), [], ["half"], 96)
-    dve(lambda e: e.memset(T.c16[:], 2.0 ** -16), [], ["c16"], 16)
-    dve(lambda e: e.memset(T.pool[:, 0:BASE], 0.0), [], ["poolA"], BASE)
-    dve(lambda e: e.memset(T.pool[:, BASE + V:], 0.0), [], ["poolB"], W - V)
-    dve(lambda e: e.memset(T.hz[:, 0:C], 0.0), [], ["hz0"], C)
-    dve(lambda e: e.memset(T.qn[:, C:], -1.0), [], ["qn1"], C)
-    dve(lambda e: e.memset(col("lb0"), V - 1 + BASE - BIG), [], ["lb0"], 1)
-
-    def gp(fn, r, w, el):
-        op("g", fn, r, w, 170 + 2 * el * 0.83)
-
-    gp(lambda e: e.iota(T.pmi[:, 0:1], [[0, 1]], 0, 1), [], ["pmi0"], 1)
-    gp(lambda e: e.iota(T.ki[:], [[1, 16]], 0, 0, allow_small_or_imprecise_dtypes=True), [], ["ki"], 16)
-    gp(lambda e: e.affine_select(T.bd[:], T.bd[:], [[-16, 8], [0, 16]], A.is_ge, 0.0, 0, 1), ["bd"], ["bd"], 128)
-    gp(lambda e: e.affine_select(T.bd[:], T.bd[:], [[16, 8], [0, 16]], A.is_ge, 0.0, 15, -1), ["bd"], ["bd"], 128)
+    lb_ = [0, 896, 1792, 2688, 3072]
+    dma("sp", T.sgi[:, 0:1], T.sg[:], [], ["sgi"])
+    dma("act", T.sti[:], T.st0[:], [], ["sti"])
+    dma("act", T.cxb[:, 0:C], T.cx0[:, 0:C], [], ["cxb0"])
+    for i in range(4):
+        dma("sp" if i % 2 == 0 else "act", T.raw[:, lb_[i]:lb_[i + 1]], T.recs[:, lb_[i]:lb_[i + 1]], [], ["raw%d" % i])
+    dma("sp", T.cxb[:, C:], T.cx0[:, C:], [], ["cxb1", "cxb2"])
+    fill(T.bd[:], 1.0, ["bd"]); fill(T.wb[:, 0:2], 0.0, ["wb_x", "wb_x2"]); fill(T.wf[:, 0:1], 0.0, ["wf_i"])
+    fill(T.wb[:, 2:], 0.0, ["wb_" + k for k in BFW[2:]]); fill(T.wf[:, 1:], 0.0, ["wf_" + k for k in F32W[1:]])
+    fill(T.wl[:], 0.0, ["wl"]); fill(T.zero[:], 0.0, ["zero"]); fill(T.half[:], 0.5, ["half"]); fill(T.c16[:], 2.0 ** -16, ["c16"])
+    fill(T.pool[:, 0:BASE], 0.0, ["poolA"]); fill(T.pool[:, BASE + V:], 0.0, ["poolB"]); fill(T.hz[:, 0:C], 0.0, ["hz0"])
+    fill(T.qn[:, C:], -1.0, ["qn1"]); fill(col("lb0"), V - 1 + BASE - BIG, ["lb0"])
+    op("g", lambda e: e.iota(T.pmi[:, 0:1], [[0, 1]], 0, 1), [], ["pmi0"])
+    iota(T.ki[:], [[1, 16]], 0, ["ki"])
+    sel(T.bd[:], [[-16, 8], [0, 16]], A.is_ge, 0.0, 0, 1, "bd")
+    sel(T.bd[:], [[16, 8], [0, 16]], A.is_ge, 0.0, 15, -1, "bd")
 
     def entry(buf, names, k, src, lo, hi, val, diag=False, step=1):
-        ap = T[buf][:, names.index(k), :, lo:hi:step]
-        m = len(range(lo, hi, step))
-        gp(lambda e: e.affine_select(ap, ap, [[-16, 8], [-1 if diag else 0, m]], A.not_equal, float(val), -src, 1),
-           [buf + "_" + k], [buf + "_" + k], 8 * m)
+        sel(T[buf][:, names.index(k), :, lo:hi:step], [[-16, 8], [-1 if diag else 0, len(range(lo, hi, step))]], A.not_equal, val, -src, 1, buf + "_" + k)
 
     def eb_(*a, **kw):
         entry("wb", BFW, *a, **kw)
@@ -152,14 +136,13 @@ def build(T, topo, core, opt):
     eb_("x", 0, 0, 12, 0.5, diag=True); eb_("x", 15, 0, 12, -0.5); eb_("x", 15, 12, 16, 1 / 256)
     eb_("x2", 0, 0, 12, 0.5, diag=True); eb_("x2", 15, 0, 12, 255 / 512); eb_("x2", 15, 12, 16, 255 / 256)
     idw = W // 8
-    gp(lambda e: e.iota(T.ident[:, 0:idw], [[1, idw]], 0, 0, allow_small_or_imprecise_dtypes=True), [], ["id0"], idw)
-    gp(lambda e: e.iota(T.dum[:], [[-C, 2], [16, 12]], C, 0, allow_small_or_imprecise_dtypes=True), [], ["dum"], 24)
+    iota(T.ident[:, 0:idw], [[1, idw]], 0, ["id0"])
+    iota(T.dum[:], [[-C, 2], [16, 12]], C, ["dum"])
     for i, val in ((0, 1.0), (1, BIG)):
-        gp(lambda e, i=i, val=val: e.affine_select(T.wl[:, 15:143:16], T.wl[:, 15:143:16], [[-16, 8]], A.not_equal, val, -i, 1), ["wl"], ["wl"], 8)
+        sel(T.wl[:, 15:143:16], [[-16, 8]], A.not_equal, val, -i, 1, "wl")
     ef_("rs", 14, 2, 4, 1.0, diag=True); ef_("rs", 14, 4, 6, -1.0, diag=True)
     ef_("rs", 12, 6, 9, 1.0, diag=True, step=2); ef_("rs", 12, 7, 10, -1.0, diag=True, step=2)
     ef_("sr", 0, 6, 10, -1.0, step=2); ef_("sr", 0, 7, 10, 1.0, step=2)
-    eb_("b", 14, 14, 16, 0.5, diag=True)
     eb_("sg", 15, 2, 6, K, step=2); eb_("sg", 15, 3, 6, -K, step=2)
     eb_("sg", 15, 6, 10, K, step=3); eb_("sg", 15, 7, 9, -K); eb_("win", 0, 10, 11, 1.0)
     ef_("rt", 14, 4, 6, 1.0); ef_("rt", 15, 4, 6, 1.0)
@@ -168,93 +151,76 @@ def build(T, topo, core, opt):
     eb_("q", 0, 12, 14, 1.0); eb_("q", 1, 12, 14, BIG)
     eb_("qs", 15, 12, 13, -K2); eb_("qs", 15, 13, 14, K2)
     eb_("tot", 0, 0, 16, 1.0)
-
-    def ts(out, in0, s1, s2, o0, o1, r, w, el=1):
-        if o1 is None:
-            dve(lambda e: e.tensor_scalar(out, in0, s1, None, o0), r, w, el)
-        else:
-            dve(lambda e: e.tensor_scalar(out, in0, s1, s2, o0, o1), r, w, el)
-
-    def lin(out, in_, scale, bias, r, w, el=1, banks=(), f=F.Identity):
-        act(lambda e: e.activation(out, in_, f, bias=bias, scale=scale), r, w, el, banks)
-
     ts(T.pmi[:, 1:2], T.pmi[:, 0:1], 15, None, A.bitwise_and, None, ["pmi0"], ["pmi1"])
-    dve(lambda e: e.tensor_copy(col("pm"), T.pmi[:, 1:2]), ["pmi1"], ["pm"], 1)
+    cp(col("pm"), T.pmi[:, 1:2], ["pmi1"], ["pm"])
     ts(T.oh[:], T.ki[:], col("pm"), None, A.is_equal, None, ["ki", "pm"], ["oh"])
-    dve(lambda e: e.tensor_tensor(T.oh2[:], T.oh[:, 0:16:2], T.oh[:, 1:16:2], A.add), ["oh"], ["oh2"], 16)
+    tt(T.oh2[:], T.oh[:, 0:16:2], T.oh[:, 1:16:2], A.add, ["oh"], ["oh2"])
     lin(col("cs"), col("pm"), -400.0, 5400.0, ["pm"], ["cs0"], f=F.Sigmoid)
     ts(col("cs1"), col("cs"), 0.5, None, A.is_gt, None, ["cs0"], ["cs"])
     lin(col("cb"), oh2(6), -2048.0, oh(15), ["oh", "oh2"], ["cb"])
-    dve(lambda e: e.tensor_copy(col("e"), T.sgi[:, 0:1]), ["sgi"], ["e"], 1)
+    cp(col("e"), T.sgi[:, 0:1], ["sgi"], ["e"])
     lin(col("z"), oh(15), -0.5, col("e"), ["oh", "e"], ["z"])
     g8 = T.bd[:, :, 0]
     ts(T.wz[:, 0:8], g8, col("z"), -1.0, A.mult, A.mult, ["bd", "z"], ["wz0"])
     ts(T.wz[:, 8:16], g8, col("z"), None, A.mult, None, ["bd", "z"], ["wz1"])
     ts(T.wz[:, 16:24], g8, oh(12), None, A.mult, None, ["bd", "oh"], ["wz2"])
     ts(T.wz[:, 24:32], g8, oh(13), None, A.mult, None, ["bd", "oh"], ["wz3"])
-    dve(lambda e: e.tensor_copy(T.ih[:], T.wf[:, 0]), ["wf_i"], ["ih"], 128)
+    cp(T.ih[:], T.wf[:, 0], ["wf_i"], ["ih"])
     for c in range(3):
-        dve(lambda e, c=c: e.tensor_copy(T["lz%d" % c][:], T.zero[:]), ["zero"], ["lz%d" % c], 136)
-    dve(lambda e: e.tensor_copy(T.wr1[:], T.zero[:, 0:128]), ["zero"], ["wr1"], 64)
+        cp(T["lz%d" % c][:], T.zero[:], ["zero"], ["lz%d" % c])
+    cp(T.wr1[:], T.zero[:, 0:128], ["zero"], ["wr1"])
+    cp(T.wsr[:], wf["sr"], ["wf_sr"], ["wsr"])
     ts(T.wr1[:, :, 14], g8, col("z"), -1.0, A.mult, A.mult, ["bd", "z", "wr1"], ["wr1"])
     ts(T.wr1[:, :, 15], g8, col("z"), None, A.mult, None, ["bd", "z", "wr1"], ["wr1"])
-    lin(col("h14"), oh2(7), 0.5, 0.0, ["oh2"], ["h14"])
     for i in range(1, 8):
-        lin(T.ident[:, i * idw:(i + 1) * idw], T.ident[:, 0:idw], 1.0, float(i * idw), ["id0"], ["id%d" % i], idw)
+        lin(T.ident[:, i * idw:(i + 1) * idw], T.ident[:, 0:idw], 1.0, float(i * idw), ["id0"], ["id%d" % i])
     ids = ["id%d" % i for i in range(8)]
-    lin(T.dum[:], T.dum[:], 1.0, col("pm"), ["dum", "pm"], ["dum"], 24)
-    lin(T.wb[:, BFW.index("c"), :, 0:2], T.bd[:, :, 0:2], -1.0, 0.0, ["bd", "wb_c"], ["wb_c"], 16)
+    lin(T.dum[:], T.dum[:], 1.0, col("pm"), ["dum", "pm"], ["dum"])
+    lin(T.wb[:, BFW.index("c"), :, 0:2], T.bd[:, :, 0:2], -1.0, 0.0, ["bd", "wb_c"], ["wb_c"])
     ts(col("ws0"), col("pm"), 10.5, 0.5, A.is_lt, A.mult, ["pm"], ["ws0"])
     lin(col("ws"), oh(1), -0.5, col("ws0"), ["oh", "ws0"], ["ws"])
-    lin(wb["s"], T.bd[:], col("ws"), 0.0, ["bd", "ws", "wb_s"], ["wb_s"], 128)
+    lin(wb["s"], T.bd[:], col("ws"), 0.0, ["bd", "ws", "wb_s"], ["wb_s"])
     lin(col("r0"), oh2(1), K - 3.5, 0.0, ["oh2"], ["r0"])
     lin(col("r1"), oh2(2), K - 32.5, col("r0"), ["oh2", "r0"], ["r1"])
-    lin(col("r3"), oh(6), K - 0.5, col("r1"), ["oh", "r1"], ["r3"])
-    lin(col("r4"), oh(7), -K - 0.5, col("r3"), ["oh", "r3"], ["r4"])
-    lin(col("r5"), oh(8), K - 0.5, col("r4"), ["oh", "r4"], ["r5"])
-    lin(col("r2"), oh(9), -K - 0.5, col("r5"), ["oh", "r5"], ["r2"])
+    lin(col("r3"), oh(6), K - 2048.5, col("r1"), ["oh", "r1"], ["r3"])
+    lin(col("r4"), oh(7), -K + 2047.5, col("r3"), ["oh", "r3"], ["r4"])
+    lin(col("r5"), oh(8), K - 2048.5, col("r4"), ["oh", "r4"], ["r5"])
+    lin(col("r2"), oh(9), -K + 2047.5, col("r5"), ["oh", "r5"], ["r2"])
     lin(col("hb"), oh2(7), -MAG, 0.0, ["oh2"], ["hb"])
     lin(col("qb0"), oh2(6), V - BIG - K2, -1.0, ["oh2"], ["qb0"])
     ts(col("os"), col("pm"), 11.5, 0.5, A.is_lt, A.mult, ["pm"], ["os"])
     lin(col("ob"), col("os"), -256.0, 0.0, ["os"], ["ob"])
     lin(col("d0"), oh(1), -1.0, 1.0, ["oh"], ["d0c"])
-    lin(T.d0[:], T.zero[:, 0:C], 1.0, col("d0"), ["zero", "d0c"], ["d0"], C)
+    lin(T.d0[:], T.zero[:, 0:C], 1.0, col("d0"), ["zero", "d0c"], ["d0"])
     lin(col("t0"), oh(0), -2.5 * 2.0 ** 97, 0.0, ["oh"], ["t0"])
-    dve(lambda e: e.tensor_tensor_scan(T.thr[:], T.half[:], T.zero[:, 0:C], col("t0"), A.mult, A.add), ["half", "zero", "t0"], ["thr"], 96)
+    scan(T.thr[:], T.half[:], T.zero[:, 0:C], col("t0"), ["half", "zero", "t0"], ["thr"])
     ts(T.lt[:], T.ki[:], col("pm"), -0.5, A.is_lt, A.mult, ["ki", "pm"], ["lt"])
-    lin(T.lt[:], T.lt[:], 1.0, 1.0, ["lt"], ["lt"], 16)
-    dve(lambda e: e.tensor_tensor_scan(T.ww[:, 0:16], T.lt[:], T.zero[:, 0:16], 2.0 ** 96, A.mult, A.add), ["lt", "zero"], ["ww0"], 16)
-    dve(lambda e: e.tensor_tensor_scan(T.ww[:, 16:27], T.c16[:, 0:11], T.zero[:, 0:11], T.ww[:, 15:16], A.mult, A.add), ["c16", "zero", "ww0"], ["ww1"], 16)
+    lin(T.lt[:], T.lt[:], 1.0, 1.0, ["lt"], ["lt"])
+    scan(T.ww[:, 0:16], T.lt[:], T.zero[:, 0:16], 2.0 ** 96, ["lt", "zero"], ["ww0"])
+    scan(T.ww[:, 16:27], T.c16[:, 0:11], T.zero[:, 0:11], T.ww[:, 15:16], ["c16", "zero", "ww0"], ["ww1"])
     ww = ["ww0", "ww1"]
-    dve(lambda e: e.tensor_copy(T.ix0[:], T.sti[:]), ["sti"], ["ix0"], 64)
+    cp(T.ix0[:], T.sti[:], ["sti"], ["ix0"])
     for c, (o, m) in enumerate(CH):
-        lin(T.y0[:, o:o + m], T.cxb[:, o:o + m], 2.0, 256.0, ["cxb%d" % c], ["y0_%d" % c], m)
-    for i in range(LOADS):
-        dve(lambda e, i=i: e.tensor_copy(T.pool[:, BASE + lb_[i]:BASE + lb_[i + 1]], T.raw[:, lb_[i]:lb_[i + 1]]),
-            ["raw%d" % i], ["pool%d" % i], lb_[i + 1] - lb_[i])
-    allpool = ["poolA", "poolB"] + ["pool%d" % i for i in range(LOADS)]
+        lin(T.y0[:, o:o + m], T.cxb[:, o:o + m], 2.0, 256.0, ["cxb%d" % c], ["y0_%d" % c])
+    for i in range(4):
+        cp(T.pool[:, BASE + lb_[i]:BASE + lb_[i + 1]], T.raw[:, lb_[i]:lb_[i + 1]], ["raw%d" % i], ["pool%d" % i])
+    allpool = ["poolA", "poolB"] + ["pool%d" % i for i in range(4)]
 
     def store0(v):
-        a, b = opt["store0"][v]
-        if b > a:
-            dma("sp", T.yp[:, a:b], T.pool[:, BASE + a:BASE + b], allpool + ["PW", "PC"], ["yp%d" % v], 512 * (b - a))
+        a, b = [(0, 2048), (2048, V)][v]
+        dma("sp", T.yp[:, a:b], T.pool[:, BASE + a:BASE + b], allpool + ["PW", "PC", "i1_1"], ["yp%d" % v])
 
     def bank(c, i):
         return T["pb%d" % (2 * c + i)], "B%d" % (2 * c + i)
 
     t0, t1 = T.pb6, T.pb7
 
-    def yin(v, c):
-        if v == 0:
-            return ["y0_%d" % c]
-        return ["y%d_%d" % (v, c)] + [["arr:y%d_a" % v], ["arr:y%d_1" % v, "arr:y%d_0" % v], ["arr:y%d_2" % v]][c]
-
     def xpass(v, c, first, which):
         o, m = CH[c]
         p, b = bank(c, which)
         k = ("x", "x2")[which]
-        pe([(p[:, 0:m], wb[k], T["y%d" % v][:, o:o + m], True, True, m)],
-           ["wb_" + k] + (yin(v, c) if first else ["y%d_%d" % (v, c)]), ["p%s%d" % (k, c)], [b])
+        arr = [["arr:y%d_a" % v], ["arr:y%d_1" % v, "arr:y%d_0" % v], ["arr:y%d_2" % v]][c] if first and v else []
+        pe([(p[:, 0:m], wb[k], T["y%d" % v][:, o:o + m], True, True)], ["wb_" + k, "y%d_%d" % (v, c)] + arr, ["p%s%d" % (k, c)], [b])
 
     def gather(v, c, k):
         o, m = CH[c]
@@ -265,18 +231,16 @@ def build(T, topo, core, opt):
             r = ["ix0"]
         else:
             r = [["arr:i%d_1" % v], ["arr:i%d_1" % v, "arr:i%d_0" % v], ["arr:i%d_2" % v]][c]
-        act(lambda e: e.activation(T.rec[:, o:o + m], pw.indirect(src[:, o // 16:(o + m) // 16]), F.Identity, bias=col("cb"), scale=col("cs1")),
-            r + allpool + ["PW", "cb", "cs"], ["rec%d" % c], 60 + GA * m)
+        lin(T.rec[:, o:o + m], pw.indirect(src[:, o // 16:(o + m) // 16]), col("cs1"), col("cb"), r + allpool + ["PW", "cb", "cs"], ["rec%d" % c])
         ops[-1]["lock"] = "r"
 
     def step(v, c, k):
         o, m = CH[c]
         (p0, b0), (p1, b1) = bank(c, 0), bank(c, 1)
         y = T["y%d" % v]
-        rc, pc, yc, xc, x2c = T.rec[:, o:o + m], T.pr[:, o:o + m], y[:, o:o + m], p0[:, 0:m], p1[:, 0:m]
-        dve(lambda e: e.tensor_tensor(pc, rc, xc, A.mult), ["rec%d" % c, "px%d" % c], ["pr%d" % c], m, [b0])
-        dve(lambda e: e.tensor_tensor(yc, rc, x2c, A.add), ["rec%d" % c, "px2%d" % c], ["y%d_%d" % (v, c)], m, [b1])
-        both = c > 0 and k in opt["merge"]
+        tt(T.pr[:, o:o + m], T.rec[:, o:o + m], p0[:, 0:m], A.mult, ["rec%d" % c, "px%d" % c], ["pr%d" % c], [b0])
+        tt(y[:, o:o + m], T.rec[:, o:o + m], p1[:, 0:m], A.add, ["rec%d" % c, "px2%d" % c], ["y%d_%d" % (v, c)], [b1])
+        both = c > 0 and k < 2
         if both:
             xpass(v, c, False, 1)
             if c == 1:
@@ -286,139 +250,131 @@ def build(T, topo, core, opt):
             (p0, b0), (p1, b1) = bank(c, 0), bank(c, 1)
         M, a0, na = m // 8, o // 16, m // 16
         lz, mk = T["lz%d" % c], T["mk%d" % c]
-        pe([(p0[0:M, q:256:8], T.pr[:, o + q:o + m:8], T.wz[:], True, True, max(min(M, 64), 32)) for q in range(8)],
+        pe([(p0[0:M, q:256:8], T.pr[:, o + q:o + m:8], T.wz[:], True, True) for q in range(8)],
            ["pr%d" % c, "wz0", "wz1", "wz2", "wz3"] + (["pr2"] if both else []), ["px%d" % c], [b0])
         if k < 2 and not both:
             xpass(v, c, False, 1)
-        lin(mk[0:M, :], p0[0:M, 0:128], 400.0, 0.0, ["px%d" % c], ["mk%d" % c], 128, [b0], f=F.Sigmoid)
-        dve(lambda e: e.tensor_tensor(lz[0:M, 1:32:2, :], mk[0:M, :], p0[0:M, 128:256], A.mult), ["mk%d" % c, "px%d" % c], ["lz%d" % c], 128, [b0])
+        lin(mk[0:M, :], p0[0:M, 0:128], 400.0, 0.0, ["px%d" % c], ["mk%d" % c], [b0], f=F.Sigmoid)
+        tt(lz[0:M, 1:32:2, :], mk[0:M, :], p0[0:M, 128:256], A.mult, ["mk%d" % c, "px%d" % c], ["lz%d" % c], [b0])
         lo = p1[:, 416:416 + na]
-        pe([(lo, lz[0:M, 16 * (q // 2) + 1 - q % 2:16 * (q // 2) + 17 - q % 2, :], T.ih[0:M, q % 2:M:2], q == 0, q == 3, 64) for q in range(4)],
+        pe([(lo, lz[0:M, 16 * (q // 2) + 1 - q % 2:16 * (q // 2) + 17 - q % 2, :], T.ih[0:M, q % 2:M:2], q == 0, q == 3) for q in range(4)],
            ["lz%d" % c, "ih"], ["lo%d" % c], [b1])
         if k < 2:
             xpass(v, c, False, 0)
         if k == 2 and v == 2 and c > 0:
-            lin(T.fs[:, a0:a0 + na], lo, 1.0, 2048.0, ["lo%d" % c], ["fs%d" % c], na, [b1])
+            lin(T.fs[:, a0:a0 + na], lo, 1.0, 2048.0, ["lo%d" % c], ["fs%d" % c], [b1])
         else:
             dst = (T.i1, T.i2, T["io%d" % v])[k]
             nm = "i%d_%d" % (k + 1, c) if k < 2 else "io%d_%d" % (v, c)
-            dve(lambda e: e.tensor_scalar(dst[:, a0:a0 + na], lo, 2048.0, None, A.add), ["lo%d" % c], [nm] + (["i%d_2" % (k + 1)] if both else []), na, [b1])
+            ts(dst[:, a0:a0 + na], lo, 2048.0, None, A.add, None, ["lo%d" % c], [nm] + (["i%d_2" % (k + 1)] if both else []), [b1])
         if c == 0 and k == 1:
-            lin(T.sf[:], lo, 1.0, 2048.0, ["lo0"], ["sf"], 12, [b1])
-            lin(T.el1[:], lo, 1.0, 2048.0 + BASE - 1 - BIG, ["lo0"], ["el1"], 12, [b1])
+            lin(T.sf[:], lo, 1.0, 0.0, ["lo0"], ["sf"], [b1])
+            lin(T.el1[:], lo, 1.0, 2048.0 + BASE - 1 - BIG, ["lo0"], ["el1"], [b1])
         if c == 0 and k == 2:
-            lin(T.tf[:], lo, 1.0, 2048.0, ["lo0"], ["tf"], 12, [b1])
-            lin(T.el2[:, 12:24], lo, 1.0, 2048.0 + BASE - 1 - BIG, ["lo0"], ["el2b"], 12, [b1])
-            lin(T.tb[:], lo, 1.0, 2048.0 + BASE, ["lo0"], ["tb"], 12, [b1])
+            lin(T.tf[:], lo, 1.0, 0.0, ["lo0"], ["tf"], [b1])
+            lin(T.el2[:, 12:24], lo, 1.0, 2048.0 + BASE - 1 - BIG, ["lo0"], ["el2b"], [b1])
+            lin(T.tb[:], lo, 1.0, 2048.0 + BASE, ["lo0"], ["tb"], [b1])
         if k == 2:
             no = (416, 0, 608)[c]
             if v < 2:
                 if c == 1:
-                    send(1, T["y%d" % (v + 1)][:, 0:C], y[:, o:o + C], ["y%d_1" % v], "y%d_a" % (v + 1), 256 * C)
-                    send(1, T["y%d" % (v + 1)][:, C:m], y[:, o + C:o + m], ["y%d_1" % v], "y%d_1" % (v + 1), 256 * m)
+                    send(1, T["y%d" % (v + 1)][:, 0:C], y[:, o:o + C], ["y%d_1" % v], "y%d_a" % (v + 1))
+                    send(1, T["y%d" % (v + 1)][:, C:m], y[:, o + C:o + m], ["y%d_1" % v], "y%d_1" % (v + 1))
                 else:
-                    send(1, T["y%d" % (v + 1)][:, no:no + m], y[:, o:o + m], ["y%d_%d" % (v, c)], "y%d_%d" % (v + 1, c), 256 * m)
+                    send(1, T["y%d" % (v + 1)][:, no:no + m], y[:, o:o + m], ["y%d_%d" % (v, c)], "y%d_%d" % (v + 1, c))
                 if c > 0:
-                    send(1, T["ix%d" % (v + 1)][:, no // 16:no // 16 + na], T["io%d" % v][:, a0:a0 + na], ["io%d_%d" % (v, c)], "i%d_%d" % (v + 1, c), 256 * na)
+                    send(1, T["ix%d" % (v + 1)][:, no // 16:no // 16 + na], T["io%d" % v][:, a0:a0 + na], ["io%d_%d" % (v, c)], "i%d_%d" % (v + 1, c))
             else:
-                lin(T.xo[:, o:o + m], y[:, o:o + m], col("os"), col("ob"), ["y2_%d" % c, "os", "ob"], ["xo%d" % c], m)
-                send(-2, T.xland[:, o:o + m], T.xo[:, o:o + m], ["xo%d" % c], "xf%d" % c, 256 * m)
+                lin(T.xo[:, o:o + m], y[:, o:o + m], col("os"), col("ob"), ["y2_%d" % c, "os", "ob"], ["xo%d" % c])
+                send(-2, T.xland[:, o:o + m], T.xo[:, o:o + m], ["xo%d" % c], "xf%d" % c)
                 for j, p, m1 in [[(384, 0, 192)], [(576, 192, 32), (0, 224, 384)], [(608, 608, 416)]][c]:
-                    dma("sp", T.yx[:, j:j + m1], T.xland[:, p:p + m1], ["arr:xf%d" % c], [], 256 * m1)
+                    dma("sp", T.yx[:, j:j + m1], T.xland[:, p:p + m1], ["arr:xf%d" % c], [])
                 if c == 2:
-                    send(-2, T.fland[:, 12:64], T.fs[:, 12:64], ["fs1", "fs2"], "ff", 512 * 52)
+                    send(-2, T.fland[:, 12:64], T.fs[:, 12:64], ["fs1", "fs2"], "ff")
                     for j, p, m1 in [(36, 12, 2), (0, 14, 24), (38, 38, 26)]:
-                        dma("sp", T.ys[:, j:j + m1], T.fland[:, p:p + m1], ["arr:ff"], [], 512 * m1)
+                        dma("sp", T.ys[:, j:j + m1], T.fland[:, p:p + m1], ["arr:ff"], [])
 
     def pick(out, win, idx, r, w):
-        act(lambda e: e.activation(out, win.indirect(idx), F.Identity), r, w, 60 + GA * C)
+        op("act", lambda e: e.activation(out, win.indirect(idx), F.Identity), r, w)
 
     def compare(row, rown, lst, lstn, wt, wtn, out, b, outn, close):
         for a in range(12):
-            ts(T.eb[:, a, 16 * a:C], row[:, 16 * a:C], lst[:, a:a + 1], wt[:, a:a + 1], A.is_equal, A.mult,
-               [rown, lstn] + wtn, ["eb%d" % a], C - 16 * a)
+            ts(T.eb[:, a, 16 * a:C], row[:, 16 * a:C], lst[:, a:a + 1], wt[:, a:a + 1], A.is_equal, A.mult, [rown, lstn] + wtn, ["eb%d" % a])
         for x in (range(0, 6), range(6, 12)):
-            pe([(out[:, 16 * u:C], wb["c"], T.eb[:, u, 16 * u:C], False, close and u == 11, max(64, C - 16 * u)) for u in x],
+            pe([(out[:, 16 * u:C], wb["c"], T.eb[:, u, 16 * u:C], False, close and u == 11) for u in x],
                ["eb%d" % u for u in x] + ["wb_c", outn], [outn], [b])
 
-    def tolist(out, early, rhs):
-        return [(out, wf["i"], early, True, False, 256)] + [(out, T.wl[:, 15 - r:143 - r], rhs(r), False, r == 15, 64) for r in range(16)]
+    def tolist(out, first, rhs):
+        return [(out, wf["i"], first, True, False)] + [(out, T.wl[:, 15 - r:143 - r], rhs(r), False, r == 15) for r in range(16)]
 
     def early(v):
         s = T.i2[:, 0:12]
-        pick(T.srow[:], T.ident[:, 0:W], s, ["i2_0"] + ids, ["srow"])
+        ts(T.srow[:], T.ident[:, 0:W].indirect(s), -2048.0, None, A.add, None, ["i2_0"] + ids, ["srow"])
         pick(T.recs_[:], pw, s, ["i2_0", "PW", "PC"] + allpool, ["recs"])
-        pe([(t0[:, 0:C], wb["c"], T.thr[:], True, False, C)], ["wb_c", "thr"], ["r0p"], ["B6"])
+        pe([(t0[:, 0:C], wb["c"], T.thr[:], True, False)], ["wb_c", "thr"], ["r0p"], ["B6"])
         compare(T.srow, "srow", T.sf, "sf", T.ww[:, 15:27], ww, t0, "B6", "r0p", True)
-        lin(T.sg1[:], t0[:, 0:C], 1.0, 0.0, ["r0p"], ["sg1"], C, ["B6"], f=F.Sign)
+        lin(T.sg1[:], t0[:, 0:C], 1.0, 0.0, ["r0p"], ["sg1"], ["B6"], f=F.Sign)
         pe(tolist(t0[:, 192:204], T.el1[:], lambda r: T.sg1[:, r:C:16]), ["wf_i", "el1", "wl", "sg1"], ["p1"], ["B6"])
-        dve(lambda e: e.tensor_tensor(T.s1f[:], t0[:, 192:204], T.dum[:, 12:24], A.max), ["p1", "dum"], ["s1f"], 12, ["B6"])
-        dve(lambda e: e.tensor_copy(T.si[:, 0:12], T.s1f[:]), ["s1f"], ["si0"], 12)
-        lin(T.wbig[:], t0[:, 192:204], 1e29, 0.0, ["p1"], ["wbig"], 12, ["B6"], f=F.Relu)
-        dve(lambda e: e.tensor_tensor(T.w1[:], T.wbig[:], T.ww[:, 15:27], A.min), ["wbig"] + ww, ["w1"], 24)
-        lin(T.el2[:, 0:12], T.dum[:, 0:12], 0.0, col("lb%d" % v), ["dum", "lb%d" % v], ["el2a"], 12)
+        tt(T.s1f[:], t0[:, 192:204], T.dum[:, 12:24], A.max, ["p1", "dum"], ["s1f"], ["B6"])
+        cp(T.si[:, 0:12], T.s1f[:], ["s1f"], ["si0"])
+        lin(T.wbig[:], t0[:, 192:204], 1e29, 0.0, ["p1"], ["wbig"], ["B6"], f=F.Relu)
+        tt(T.w1[:], T.wbig[:], T.ww[:, 15:27], A.min, ["wbig"] + ww, ["w1"])
+        lin(T.el2[:, 0:12], T.dum[:, 0:12], 0.0, col("lb%d" % v), ["dum", "lb%d" % v], ["el2a"])
 
     def stage1(v):
-        r1, bs = t1[:, 256:448], t0[:, 256:448]
-        pe([(r1, T.wr1[:], T.pr[:, 0:C], True, True, C)], ["wr1", "pr0"], ["r1p"], ["B7"])
-        dve(lambda e: e.tensor_scalar(T.inc[:], r1, 0.0, None, A.is_gt), ["r1p"], ["inc"], C, ["B7"])
-        lin(T.sgn[:], r1, 1.0, 0.0, ["r1p"], ["sgn"], C, ["B7"], f=F.Sign)
-        pe([(t1[:, 0:C], wb["c"], T.thr[:], True, False, C), (t1[:, 0:C], wb["win"], T.sg1[:], False, False, C),
-            (t1[:, 0:C], wb["sg"], T.sgn[:], False, False, C)], ["wb_c", "thr", "wb_win", "sg1", "wb_sg", "sgn"], ["r2p"], ["B7"])
-        pe([(t1[:, 0:C], wf["sr"], T.srow[:], False, False, 4 * C)], ["wf_sr", "srow", "r2p"], ["r2p"], ["B7"])
-        pe([(t1[:, 0:C], wf["rs"], T.recs_[:], False, False, 4 * C)], ["wf_rs", "recs", "r2p"], ["r2p"], ["B7"])
-        pe([(bs, wf["i"], T.recs_[:], True, False, 4 * C), (bs, wb["b"], T.sgn[:], False, True, C)], ["wf_i", "recs", "wb_b", "sgn"], ["bsp"], ["B6"])
-        lin(T.bn[:, 0:C], bs, 1.0, col("h14"), ["bsp", "h14"], ["bn0"], C, ["B6"])
+        r1 = t1[:, 256:448]
+        pe([(r1, T.wr1[:], T.pr[:, 0:C], True, True)], ["wr1", "pr0"], ["r1p"], ["B7"])
+        lin(T.sgn[:], r1, 1.0, 0.0, ["r1p"], ["sgn"], ["B7"], f=F.Sign)
+        lin(T.inc[:], T.sgn[:], 1.0, 0.0, ["sgn"], ["inc"], f=F.Relu)
+        pe([(t1[:, 0:C], wb["c"], T.thr[:], True, False), (t1[:, 0:C], wb["win"], T.sg1[:], False, False),
+            (t1[:, 0:C], wb["sg"], T.sgn[:], False, False)], ["wb_c", "thr", "wb_win", "sg1", "wb_sg", "sgn"], ["r2p"], ["B7"])
+        pe([(t1[:, 0:C], T.wsr[:], T.srow[:], False, False)], ["wsr", "srow", "r2p"], ["r2p"], ["B7"])
+        pe([(t1[:, 0:C], wf["rs"], T.recs_[:], False, False)], ["wf_rs", "recs", "r2p"], ["r2p"], ["B7"])
 
     def scat1(v):
-        dve(lambda e: e.tensor_tensor(pall.indirect(T.si[:, 0:12]), T.recs_[:], T.inc[:], A.add), ["si0", "recs", "inc"], ["PC"], 60 + SC * C)
+        tt(pall.indirect(T.si[:, 0:12]), T.recs_[:], T.inc[:], A.add, ["si0", "recs", "inc"], ["PC"])
         ops[-1]["lock"] = "w"
         pick(T.bn[:, 2 * C:], pw, T["io%d" % v][:, 0:12], ["io%d_0" % v, "PW", "PC"], ["rect"])
+        pick(T.bn[:, 0:C], pall, T.si[:, 0:12], ["si0", "PW", "PC"], ["bn0"])
         if v == 2:
             for i in (14, 15):
-                dma("sp", T.cnt2[i:128:16, BASE:], T.pool[i:128:16, BASE:], ["PW", "PC"], ["cnt%d" % i], 120000 * (i - 13))
+                dma("sp", T.cnt2[i:128:16, BASE:], T.pool[i:128:16, BASE:], ["PW", "PC"], ["cnt%d" % i])
 
     def late(v):
-        t = T["io%d" % v][:, 0:12]
         (a0, ba0), (a1, ba1) = bank(0, 0), bank(0, 1)
-        pick(T.trow[:], T.ident[:, 0:W], t, ["io%d_0" % v] + ids, ["trow"])
+        ts(T.trow[:], T.ident[:, 0:W].indirect(T["io%d" % v][:, 0:12]), -2048.0, None, A.add, None, ["io%d_0" % v] + ids, ["trow"])
         compare(T.trow, "trow", T.tf, "tf", T.w1, ["w1"], t1, "B7", "r2p", False)
-        pe([(t1[:, 0:C], wf["rt"], T.bn[:, 2 * C:], False, True, 4 * C)], ["wf_rt", "rect", "r2p"], ["r2p"], ["B7"])
+        pe([(t1[:, 0:C], wf["rt"], T.bn[:, 2 * C:], False, True)], ["wf_rt", "rect", "r2p"], ["r2p"], ["B7"])
         r3 = a1[:, 192:384]
-        pe([(r3, wb["y"], T["y%d" % v][:, 0:C], True, False, C), (r3, wf["h"], T.bn[:, 2 * C:], False, True, 4 * C)],
+        pe([(r3, wb["y"], T["y%d" % v][:, 0:C], True, False), (r3, wf["h"], T.bn[:, 2 * C:], False, True)],
            ["wb_y", "wf_h", "rect", "y%d_0" % v], ["r3p"], [ba1])
-        lin(T.rr[:], r3, 1.0, MAG, ["r3p"], ["rr"], C, [ba1])
-        lin(T.bn[:, C:2 * C], T.rr[:], 1.0, -MAG, ["rr"], ["bn1"], C)
-        lin(T.hz[:, C:], T.rr[:], oh2(7), col("hb"), ["rr", "oh2", "hb"], ["hm"], C)
-        lin(T.fl[:], t1[:, 0:C], 1.0, col("r2"), ["r2p", "r2"], ["fl"], C, ["B7"], f=F.Sign)
-        pe([(t0[:, 0:C], wb["s"], T.fl[:], True, True, C)], ["wb_s", "fl"], ["r0p"], ["B6"])
-        lin(T.cr[:, 1], t0[:, 0:C], 1.0, -2.0, ["r0p"], ["cr1"], C, ["B6"], f=F.Relu)
-        dve(lambda e: e.tensor_tensor_scan(T.cr[:, 0], T.d0[:], T.cr[:, 1], 0.0, A.mult, A.add), ["d0", "cr1"], ["cr0"], 96)
-        pe([(a0[:, 0:C], wb["qs"], T.sgn[:], True, False, C)], ["wb_qs", "sgn"], ["px0"], [ba0])
-        pe([(a0[:, 0:C], wb["q"], T.cr[:, 0], False, True, C)], ["wb_q", "cr0", "px0"], ["px0"], [ba0])
-        pe(tolist(t0[:, 204:228], T.el2[:], lambda r: T.cr[:, :, r:C:16]), ["wf_i", "el2a", "el2b", "wl", "cr0", "cr1"], ["p2"], ["B6"])
-        lin(T.qn[:, 0:C], a0[:, 0:C], 1.0, col("qb%d" % v), ["px0", "qb%d" % v], ["qn0"], C, [ba0])
-        dve(lambda e: e.tensor_tensor(T.idf[:], t0[:, 204:228], T.dum[:], A.max), ["p2", "dum"], ["idf"], 24, ["B6"])
-        dve(lambda e: e.tensor_copy(T.si[:, 12:36], T.idf[:]), ["idf"], ["si1"], 24)
-        dve(lambda e: e.tensor_tensor(T.ncf[:], T.idf[:, 0:12], T.tb[:], A.max), ["idf", "tb"], ["ncf"], 24)
+        lin(T.rr[:], r3, 1.0, MAG, ["r3p"], ["rr"], [ba1])
+        lin(T.bn[:, C:2 * C], T.rr[:], 1.0, -MAG, ["rr"], ["bn1"])
+        lin(T.hz[:, C:], T.rr[:], oh2(7), col("hb"), ["rr", "oh2", "hb"], ["hm"])
+        lin(T.fl[:], t1[:, 0:C], 1.0, col("r2"), ["r2p", "r2"], ["fl"], ["B7"], f=F.Sign)
+        pe([(t0[:, 0:C], wb["s"], T.fl[:], True, True)], ["wb_s", "fl"], ["r0p"], ["B6"])
+        lin(T.cr[:, 1], t0[:, 0:C], 1.0, -2.0, ["r0p"], ["cr1"], ["B6"], f=F.Relu)
+        scan(T.cr[:, 0], T.d0[:], T.cr[:, 1], 0.0, ["d0", "cr1"], ["cr0"])
+        pe([(a0[:, 0:C], wb["qs"], T.sgn[:], True, False)], ["wb_qs", "sgn"], ["px0"], [ba0])
+        pe([(a0[:, 0:C], wb["q"], T.cr[:, 0], False, True)], ["wb_q", "cr0", "px0"], ["px0"], [ba0])
+        mm = tolist(t1[:, 204:228], T.el2[:], lambda r: T.cr[:, :, r:C:16])
+        pe(mm[:1], ["wf_i", "el2a", "el2b"], ["p2"], ["B7"])
+        pe(mm[1:], ["wl", "cr0", "cr1", "p2"], ["p2"], ["B7"])
+        lin(T.qn[:, 0:C], a0[:, 0:C], 1.0, col("qb%d" % v), ["px0", "qb%d" % v], ["qn0"], [ba0])
+        tt(T.idf[:], t1[:, 204:228], T.dum[:], A.max, ["p2", "dum"], ["idf"], ["B7"])
+        cp(T.si[:, 12:36], T.idf[:], ["idf"], ["si1"])
+        tt(T.ncf[:], T.idf[:, 0:12], T.tb[:], A.max, ["idf", "tb"], ["ncf"])
         if v < 2:
-            ts(T["nc%d" % v][:], T.ncf[:], -float(BASE), None, A.add, None, ["ncf"], ["nc%d" % v], 12)
-            send(1, T["ix%d" % (v + 1)][:, 26:38], T["nc%d" % v][:], ["nc%d" % v], "i%d_0" % (v + 1), 256 * 12)
-            pe([(t1[:, 256:257], wb["tot"], T.cr[:, 0, C - 1:C], True, True, 64)], ["wb_tot", "cr0"], ["totp"], ["B7"])
-            lin(col("qb%d" % (v + 1)), t1[:, 256:257], oh2(6), col("qb%d" % v), ["totp", "oh2", "qb%d" % v], ["qb%d" % (v + 1)], 1, ["B7"])
-            lin(col("lb%d" % (v + 1)), t1[:, 256:257], 1.0, col("lb%d" % v), ["totp", "lb%d" % v], ["lb%d" % (v + 1)], 1, ["B7"])
+            ts(T["nc%d" % v][:], T.ncf[:], -float(BASE), None, A.add, None, ["ncf"], ["nc%d" % v])
+            send(1, T["ix%d" % (v + 1)][:, 26:38], T["nc%d" % v][:], ["nc%d" % v], "i%d_0" % (v + 1))
+            pe([(t0[:, 256:257], wb["tot"], T.cr[:, 0, C - 1:C], True, True)], ["wb_tot", "cr0"], ["totp"], ["B6"])
+            lin(col("qb%d" % (v + 1)), t0[:, 256:257], oh2(6), col("qb%d" % v), ["totp", "oh2", "qb%d" % v], ["qb%d" % (v + 1)], ["B6"])
+            lin(col("lb%d" % (v + 1)), t0[:, 256:257], 1.0, col("lb%d" % v), ["totp", "lb%d" % v], ["lb%d" % (v + 1)], ["B6"])
         else:
-            lin(T.fs[:, 0:12], T.ncf[:], 1.0, -float(BASE), ["ncf"], ["fs0"], 12)
-            send(-2, T.fland[:, 0:12], T.fs[:, 0:12], ["fs0"], "f0", 512 * 12)
-            dma("sp", T.ys[:, 24:36], T.fland[:, 0:12], ["arr:f0"], [], 512 * 12)
-        dve(lambda e: e.tensor_tensor(pall.indirect(T.si[:, 0:24]), T.bn[:, 0:2 * C], T.qn[:], A.max),
-            ["si0", "si1", "bn0", "bn1", "qn0", "qn1"], ["PW", "PC"], 60 + SC * 2 * C)
-
-    def scat_t():
-        pick(T.g2[:], pall, T.si[:, 24:36], ["si1", "PW", "PC"], ["g2"])
-        dve(lambda e: e.tensor_tensor(pall.indirect(T.si[:, 24:36]), T.g2[:], T.hz[:, C:], A.subtract),
-            ["si1", "g2", "hm"], ["PC"], 60 + SC * C)
-        ops[-1]["lock"] = "w"
+            lin(T.fs[:, 0:12], T.ncf[:], 1.0, -float(BASE), ["ncf"], ["fs0"])
+            send(-2, T.fland[:, 0:12], T.fs[:, 0:12], ["fs0"], "f0")
+            dma("sp", T.ys[:, 24:36], T.fland[:, 0:12], ["arr:f0"], [])
+        tt(pall.indirect(T.si[:, 0:24]), T.bn[:, 0:2 * C], T.qn[:], A.max, ["si0", "si1", "bn0", "bn1", "qn0", "qn1"], ["PW", "PC"])
 
     for v in range(3):
         if v == 0:
@@ -428,8 +384,9 @@ def build(T, topo, core, opt):
             xpass(v, c, True, 1)
         gather(v, 0, 0); step(v, 0, 0)
         if v > 0:
-            scat_t()
-            store0(v)
+            pick(T.g2[:], pall, T.si[:, 24:36], ["si1", "PW", "PC"], ["g2"])
+            tt(pall.indirect(T.si[:, 24:36]), T.g2[:], T.hz[:, C:], A.subtract, ["si1", "g2", "hm"], ["PC"])
+            ops[-1]["lock"] = "w"
         gather(v, 0, 1); step(v, 0, 1)
         early(v)
         gather(v, 0, 2); step(v, 0, 2)
@@ -437,17 +394,18 @@ def build(T, topo, core, opt):
         for k in range(3):
             for c in (1, 2):
                 gather(v, c, k); step(v, c, k)
+            if k == 0 and v == 1:
+                store0(v)
         scat1(v)
         late(v)
-    dve(lambda e: e.tensor_tensor(T.cnt2[:, 0:BASE + W].indirect(T.si[:, 12:36]), T.bn[:, C:], T.hz[:], A.subtract),
-        ["si1", "bn1", "rect", "hm", "hz0", "cnt14", "cnt15"], ["cnt"], 60 + SC * 2 * C)
-    yps = ["yp0", "yp1", "yp2"]
+    tt(T.cnt2[:, 0:BASE + W].indirect(T.si[:, 12:36]), T.bn[:, C:], T.hz[:], A.subtract, ["si1", "bn1", "rect", "hm", "hz0", "cnt14", "cnt15"], ["cnt"])
+    yps = ["yp0", "yp1"]
     for i in range(8):
-        dma("act" if i % 2 else "sp", T.yp[16 * i:16 * i + 12, V:W], T.pool[16 * i:16 * i + 12, BASE + V:], ["PW", "PC"], [], 30000 * (i + 1))
+        dma("act" if i % 2 else "sp", T.yp[16 * i:16 * i + 12, V:W], T.pool[16 * i:16 * i + 12, BASE + V:], ["PW", "PC"], [])
     for i in (12, 13):
-        dma("sp", T.yp[i:128:16, :], T.pool[i:128:16, BASE:], ["PW", "PC"] + yps, [], 240000 + 120000 * (i - 11))
+        dma("sp" if i == 12 else "act", T.yp[i:128:16, :], T.pool[i:128:16, BASE:], ["PW", "PC"] + yps, [])
     for i in (14, 15):
-        dma("sp" if i == 14 else "act", T.yp[i:128:16, :], T.cnt2[i:128:16, BASE:], ["cnt"] + yps, [], 200000 + 120000 * (i - 13))
+        dma("sp" if i == 14 else "act", T.yp[i:128:16, :], T.cnt2[i:128:16, BASE:], ["cnt"] + yps, [])
     return ops
 
 
@@ -471,7 +429,8 @@ def edges(ops):
         d.pop(i, None)
         deps.append(d)
         for x in o["r"]:
-            readers.setdefault(x, []).append(i)
+            if not (o["kind"] == "dma" and x == "i1_1"):
+                readers.setdefault(x, []).append(i)
         for x in o["w"]:
             lastw[x] = i
             readers[x] = []
@@ -505,16 +464,15 @@ def waits(ops, deps, order):
     return need
 
 
-OPT = {"par": (1.0, 0.5, 1.56, 3.8, 2500), "loads": [0, 896, 1792, 2688, 3072], "store0": [(0, 2048), (2048, 3072), (0, 0)], "merge": [0, 1],
-       "order": "05060h0x0304070100020i0n0e2a0g0y230m0a0b2e0q2c22171w1c342d1p181q191r2b1s1a30240f1b1v092f080k0o0l260c2g0p3135320r331t1x382i0s2h2y4s2s2w0t2x0u2m1u3d2n201y211z2t0v2z29272o28472p0d0w2j0j2k252l0z2u3e102q2r39152v161f1d111e1k1l1g3a1213141m3b1h1i3c3j5h1j3l3k1n3n1o3m373o3h363p3q5i5d3f3s3r3i3t3g5e3u5m3v5f3w5n3x3y5o5g3z5j4041425p5q455r5l43445k4t4b4c485s4a4u4j4i4w4d495w554h4e4k4g4f5t4x4l465x4m4v6156545u4n57624y635v4o4p4z4q4r58506s5b6u5152595c6x6v6t656y6z64536w5a706671756777737274765y78796i6860696a7e7a6j6b6g6c7f6f7b6l7g6d6m7i6e5z7c7h6n6h7d7k6k6q7j7m6o7l7r7o7n8s7p7s7u7t7q9d6p7v816r7w8b7y827x838c848586879y8d88898a7z8ea0808fa2a18g8h9z8i8j8ka38l8m8na4a78o8qa5a88y8ra6a98z8xaa8p9e8uab8vac8tad8w90929594919g93ah9f9p96ae9q9h9r97ai9s989iaj9jam999a9kanaf9t9b9l9wao9m9cbd9n9obfagap9xaqbhbec3bi9uarbjasblbp9vbrbobgbqbkalbnb3bmbsataubtavb4b1buawb0axb6bzayb7c0azakb8c1b2bvc2b5c5bwbbbxbyc4c7b9c6dcc9c8bacccacfcbcdcedxbccgchcmcicjcwcncocpcxcqcrcsekctcucvckclcyeleoczd0d1emd2d3d4enepd5d6d7eqetdad8eseudedyerevddd9ewdbdfexdzdge1dhdieceye2dldpdjezdndmdodkeddqe3e0drf1e4eedse9f0f3eae5f2dtefdug9f4egdve6g5e7e8f8gxf9eifag6g7dwg8f5fbfcejfdgff6gefegaehgdgbf7gcfqgggmghgjglgiebgkfggnffgofmfrfhgtfngufsfiftgvfjgpfygwfugyfzgzh0fvgqgrfkh1fwflh2h3fxh7h4gsg1h5h8hbhahdhehihch9hghhhffofphjhkg4g3g0g2h6"}
+ORDER = "05060i0n07040m00010x02030h0e1o0k1p0f1q1s0y0b2e291t221b1r0g0917251u2z2b1v0u330a0d0q081w2t300c2d0o2f3121320v0l2i2a0j240p232c370w2x1j2g2h18342s1k4r203d1y2l1x192r1z2m272y2u1n382v462n2w1a2o2j0r2k2p281l2q0s391m0t1g3c3a1e3b3i1h361f3j1i3k5e3l1c3g153m1d3h3n165f35110z3o5a5g3p12103e3r26133q3s3f5b145h3t5i3u3v5c5j3x3w3y5k5d3z5l40415m5n42444s5o5t494i4a4t4d4c4b4v4h4754485p4g4e4f4j5v5u4k55435w4l5r5x4w564u4m4x455q534y4n5s4o4p4z5y6p505157525z58594q606q6s616r62636t786x646u726v6w746y717g736z75706f667665776c796g7a676d7c6h686i7b7d696j7i6n7e6a6k6b6l7f6e7j6m6o7q7h7l7r7k7m7n7s7o7t7p8q9b7u7v7w7x809y8182837y859u7z869z8884a0878a899va18ca29wa38d9x8ea4a58f8g8b8ha6a78ia88ja9ae8k8l8o8m9c928r908t8n8uaa8v918s8w8z8y8x939daf8p9o94ab9p9f959eajac9g9n9q96ak9hagal9i97ad98999jamba9kc19lan9m9rao9sbdap9t9abiaibebgbhahbbbfbjbkaqbqb0bpboblasbmbnarbratbcbsb1axaubtb2bxaybyb8buavc3bzawb3bvazc0bwc4b4b5c2c6b6c5cbc7b7cecccdb9dbdwcgcfcic8chclc9cacvcmcncocwcpcqckcjcrelcsctcucxenczeheocyemd1d0d2eiepd3ejeqd4erd5d6ekesdad9eteud7dxevdfdhdgdcf0dedidddjdkdmdodndydlewf2e0dpf1f3dqebeyd8e1f4ecdrdze2edexe8eze9dsf5dtdug2gvf6e3eeeff7egdvg4g5e4g6g7f8g3f9fae5e6fbgig8gbgagdg9gcgggegfgkfnghgjfdglfceae7gmfjfpgngrfkfofvgsgxgtfqfwgofegufrgygqfsffgpfggwh0ftgzfhh2h1fufih6h3fyh4h7hchhhghdhehfhahbfmh9flh8fxhjhig1fzg0h5"
 
 
 def rank_program(g, core, T, topo):
     if T.rank_of(core) is None:
         return
-    ops = build(T, topo, core, OPT)
+    ops = build(T, topo, core)
     deps = edges(ops)
-    order = [int(OPT["order"][i:i + 2], 36) for i in range(0, len(OPT["order"]), 2)]
+    order = [int(ORDER[i:i + 2], 36) for i in range(0, len(ORDER), 2)]
     seen = {"r": [], "w": []}
     for i in order:
         k = ops[i]["lock"]

from concourse.mybir import AluOpType as A, ActivationFunctionType as F

V, S, C, W = 3072, 1024, 192, 3648
BASE = 384
K, BIG, K2, MAG = 8192.0, 4096.0, 2048.0, 12582912.0
CH = [(0, 192), (192, 416), (608, 416)]
BFW = ["x", "x2", "y", "sg", "win", "c", "s", "q", "qs", "tot"]
F32W = ["i", "rs", "sr", "rt", "h"]

SCRATCH = {}
for _d, _l in {
    "int32": [("raw", [V]), ("sgi", [4]), ("sti", [64]), ("pmi", [2])],
    "float32": [("pool", [BASE + W]), ("cnt2", [BASE + W]), ("ident", [W]), ("rec", [S]), ("wf", [5, 8, 16]), ("c16", [16]), ("ki", [16]),
                ("oh", [16]), ("oh2", [8]), ("lt", [16]), ("ww", [28]), ("col", [40]), ("dum", [24]), ("sf", [12]), ("tf", [12]), ("tb", [12]),
                ("el1", [12]), ("el2", [24]), ("recs_", [C]), ("g2", [C]), ("s1f", [12]), ("wbig", [12]), ("w1", [12]), ("idf", [24]),
                ("ncf", [12]), ("bn", [3 * C]), ("qn", [2 * C]), ("hz", [2 * C]), ("inc", [C]), ("rr", [C]), ("fs", [64]), ("fland", [64])],
    "bfloat16": [("cxb", [S]), ("wb", [10, 8, 16]), ("wl", [144]), ("bd", [8, 16]), ("zero", [272]), ("half", [C]), ("thr", [C]), ("d0", [C]),
                 ("eb", [12, C]), ("sg1", [C]), ("sgn", [C]), ("fl", [C]), ("cr", [2, C]), ("xo", [S]), ("xland", [S]),
                 ("y0", [S]), ("y1", [S]), ("y2", [S]), ("mk0", [128]), ("mk1", [128]), ("mk2", [128])],
    "float16": [("pr", [S]), ("wz", [32]), ("wr1", [8, 16]), ("ih", [128]), ("srow", [C]), ("trow", [C]), ("wsr", [8, 16]),
                ("lz0", [34, 8]), ("lz1", [34, 8]), ("lz2", [34, 8])],
    "uint16": [("i1", [64]), ("i2", [64]), ("si", [36]), ("ix0", [64]), ("ix1", [64]), ("ix2", [64]), ("io0", [64]), ("io1", [64]),
               ("io2", [64]), ("nc0", [12]), ("nc1", [12])],
}.items():
    for _n, _s in _l:
        SCRATCH[_n] = ("sbuf", [128] + _s, _d)
for _b in range(8):
    SCRATCH["pb%d" % _b] = ("psum", [128, 512], "float32")
SEMAPHORES = ["c_pe", "c_act", "c_dve", "c_g", "sent"] + ["d%d" % i for i in range(36)] + ["a%d" % i for i in range(20)]


def build(T, topo, core):
    ops = []
    n = len(T.cores)
    rank = T.rank_of(core)
    cnt = {"d": 0, "a": 0}

    def op(eng, fn, r, w, banks=(), kind="c", sem=None, inc=0):
        ops.append(dict(eng=eng, fn=fn, r=list(r), w=list(w), banks=list(banks), kind=kind, sem=sem, inc=inc, lock=None))

    def dve(fn, r, w, banks=()):
        op("dve", fn, r, w, banks)

    def pe(mms, r, w, banks):
        def fn(e):
            last = None
            for m in mms:
                last = e.matmul(*m)
            return last
        op("pe", fn, r, w, banks)

    def dma(q, out, in_, r, w):
        sem = "d%d" % cnt["d"]; cnt["d"] += 1
        op(q, lambda e: e.dma_start(out, in_), r, w, kind="dma", sem=sem, inc=16)

    def send(step, out, in_, r, name):
        dst, src = T.cores[(rank + step) % n], T.cores[(rank - step) % n]
        sem = "a%d" % cnt["a"]; cnt["a"] += 1
        rid, pid, _ = topo.addr(dst)
        m = topo.mask(core, dst)
        op("g", lambda e: e.remote_dma(out, in_, T.sem[sem], T.sem.sent, pid, rid, m), r, ["arr:" + name],
           kind="rem", sem=sem, inc=len(topo.engines(src, core)))
        ops[-1]["loc"] = len(topo.engines(core, dst))

    wb = {k: T.wb[:, i] for i, k in enumerate(BFW)}
    wf = {k: T.wf[:, i] for i, k in enumerate(F32W)}
    cols = {}

    def col(k):
        if k not in cols:
            cols[k] = len(cols)
        return T.col[:, cols[k]:cols[k] + 1]

    def oh(i):
        return T.oh[:, i:i + 1]

    def oh2(i):
        return T.oh2[:, i:i + 1]

    def fill(ap, c, w):
        dve(lambda e: e.memset(ap, c), [], w)

    def cp(out, in_, r, w):
        dve(lambda e: e.tensor_copy(out, in_), r, w)

    def tt(out, a, b, o, r, w, banks=()):
        dve(lambda e: e.tensor_tensor(out, a, b, o), r, w, banks)

    def ts(out, in0, s1, s2, o0, o1, r, w, banks=()):
        if o1 is None:
            dve(lambda e: e.tensor_scalar(out, in0, s1, None, o0), r, w, banks)
        else:
            dve(lambda e: e.tensor_scalar(out, in0, s1, s2, o0, o1), r, w, banks)

    def scan(out, a, b, ini, r, w):
        dve(lambda e: e.tensor_tensor_scan(out, a, b, ini, A.mult, A.add), r, w)

    def lin(out, in_, scale, bias, r, w, banks=(), f=F.Identity):
        op("act", lambda e: e.activation(out, in_, f, bias=bias, scale=scale), r, w, banks)

    def iota(out, pat, base, w):
        op("g", lambda e: e.iota(out, pat, base, 0, allow_small_or_imprecise_dtypes=True), [], w)

    def sel(ap, pat, o, val, base, cm, nm):
        op("g", lambda e: e.affine_select(ap, ap, pat, o, float(val), base, cm), [nm], [nm])

    pw = T.pool[:, BASE:BASE + W]
    pall = T.pool[:, 0:BASE + W]
    lb_ = [0, 896, 1792, 2688, 3072]
    dma("sp", T.sgi[:, 0:1], T.sg[:], [], ["sgi"])
    dma("act", T.sti[:], T.st0[:], [], ["sti"])
    dma("act", T.cxb[:, 0:C], T.cx0[:, 0:C], [], ["cxb0"])
    for i in range(4):
        dma("sp" if i % 2 == 0 else "act", T.raw[:, lb_[i]:lb_[i + 1]], T.recs[:, lb_[i]:lb_[i + 1]], [], ["raw%d" % i])
    dma("sp", T.cxb[:, C:], T.cx0[:, C:], [], ["cxb1", "cxb2"])
    fill(T.bd[:], 1.0, ["bd"]); fill(T.wb[:, 0:2], 0.0, ["wb_x", "wb_x2"]); fill(T.wf[:, 0:1], 0.0, ["wf_i"])
    fill(T.wb[:, 2:], 0.0, ["wb_" + k for k in BFW[2:]]); fill(T.wf[:, 1:], 0.0, ["wf_" + k for k in F32W[1:]])
    fill(T.wl[:], 0.0, ["wl"]); fill(T.zero[:], 0.0, ["zero"]); fill(T.half[:], 0.5, ["half"]); fill(T.c16[:], 2.0 ** -16, ["c16"])
    fill(T.pool[:, 0:BASE], 0.0, ["poolA"]); fill(T.pool[:, BASE + V:], 0.0, ["poolB"]); fill(T.hz[:, 0:C], 0.0, ["hz0"])
    fill(T.qn[:, C:], -1.0, ["qn1"]); fill(col("lb0"), V - 1 + BASE - BIG, ["lb0"])
    op("g", lambda e: e.iota(T.pmi[:, 0:1], [[0, 1]], 0, 1), [], ["pmi0"])
    iota(T.ki[:], [[1, 16]], 0, ["ki"])
    sel(T.bd[:], [[-16, 8], [0, 16]], A.is_ge, 0.0, 0, 1, "bd")
    sel(T.bd[:], [[16, 8], [0, 16]], A.is_ge, 0.0, 15, -1, "bd")

    def entry(buf, names, k, src, lo, hi, val, diag=False, step=1):
        sel(T[buf][:, names.index(k), :, lo:hi:step], [[-16, 8], [-1 if diag else 0, len(range(lo, hi, step))]], A.not_equal, val, -src, 1, buf + "_" + k)

    def eb_(*a, **kw):
        entry("wb", BFW, *a, **kw)

    def ef_(*a, **kw):
        entry("wf", F32W, *a, **kw)

    ef_("i", 0, 0, 16, 1.0, diag=True)
    eb_("x", 0, 0, 12, 0.5, diag=True); eb_("x", 15, 0, 12, -0.5); eb_("x", 15, 12, 16, 1 / 256)
    eb_("x2", 0, 0, 12, 0.5, diag=True); eb_("x2", 15, 0, 12, 255 / 512); eb_("x2", 15, 12, 16, 255 / 256)
    idw = W // 8
    iota(T.ident[:, 0:idw], [[1, idw]], 0, ["id0"])
    iota(T.dum[:], [[-C, 2], [16, 12]], C, ["dum"])
    for i, val in ((0, 1.0), (1, BIG)):
        sel(T.wl[:, 15:143:16], [[-16, 8]], A.not_equal, val, -i, 1, "wl")
    ef_("rs", 14, 2, 4, 1.0, diag=True); ef_("rs", 14, 4, 6, -1.0, diag=True)
    ef_("rs", 12, 6, 9, 1.0, diag=True, step=2); ef_("rs", 12, 7, 10, -1.0, diag=True, step=2)
    ef_("sr", 0, 6, 10, -1.0, step=2); ef_("sr", 0, 7, 10, 1.0, step=2)
    eb_("sg", 15, 2, 6, K, step=2); eb_("sg", 15, 3, 6, -K, step=2)
    eb_("sg", 15, 6, 10, K, step=3); eb_("sg", 15, 7, 9, -K); eb_("win", 0, 10, 11, 1.0)
    ef_("rt", 14, 4, 6, 1.0); ef_("rt", 15, 4, 6, 1.0)
    ef_("h", 0, 0, 16, 0.5, diag=True); ef_("h", 12, 12, 14, 1.0, diag=True)
    eb_("y", 0, 0, 12, 255 / 1024, diag=True); eb_("y", 15, 0, 12, -0.25); eb_("y", 15, 14, 16, -1 / 1024)
    eb_("q", 0, 12, 14, 1.0); eb_("q", 1, 12, 14, BIG)
    eb_("qs", 15, 12, 13, -K2); eb_("qs", 15, 13, 14, K2)
    eb_("tot", 0, 0, 16, 1.0)
    ts(T.pmi[:, 1:2], T.pmi[:, 0:1], 15, None, A.bitwise_and, None, ["pmi0"], ["pmi1"])
    cp(col("pm"), T.pmi[:, 1:2], ["pmi1"], ["pm"])
    ts(T.oh[:], T.ki[:], col("pm"), None, A.is_equal, None, ["ki", "pm"], ["oh"])
    tt(T.oh2[:], T.oh[:, 0:16:2], T.oh[:, 1:16:2], A.add, ["oh"], ["oh2"])
    lin(col("cs"), col("pm"), -400.0, 5400.0, ["pm"], ["cs0"], f=F.Sigmoid)
    ts(col("cs1"), col("cs"), 0.5, None, A.is_gt, None, ["cs0"], ["cs"])
    lin(col("cb"), oh2(6), -2048.0, oh(15), ["oh", "oh2"], ["cb"])
    cp(col("e"), T.sgi[:, 0:1], ["sgi"], ["e"])
    lin(col("z"), oh(15), -0.5, col("e"), ["oh", "e"], ["z"])
    g8 = T.bd[:, :, 0]
    ts(T.wz[:, 0:8], g8, col("z"), -1.0, A.mult, A.mult, ["bd", "z"], ["wz0"])
    ts(T.wz[:, 8:16], g8, col("z"), None, A.mult, None, ["bd", "z"], ["wz1"])
    ts(T.wz[:, 16:24], g8, oh(12), None, A.mult, None, ["bd", "oh"], ["wz2"])
    ts(T.wz[:, 24:32], g8, oh(13), None, A.mult, None, ["bd", "oh"], ["wz3"])
    cp(T.ih[:], T.wf[:, 0], ["wf_i"], ["ih"])
    for c in range(3):
        cp(T["lz%d" % c][:], T.zero[:], ["zero"], ["lz%d" % c])
    cp(T.wr1[:], T.zero[:, 0:128], ["zero"], ["wr1"])
    cp(T.wsr[:], wf["sr"], ["wf_sr"], ["wsr"])
    ts(T.wr1[:, :, 14], g8, col("z"), -1.0, A.mult, A.mult, ["bd", "z", "wr1"], ["wr1"])
    ts(T.wr1[:, :, 15], g8, col("z"), None, A.mult, None, ["bd", "z", "wr1"], ["wr1"])
    for i in range(1, 8):
        lin(T.ident[:, i * idw:(i + 1) * idw], T.ident[:, 0:idw], 1.0, float(i * idw), ["id0"], ["id%d" % i])
    ids = ["id%d" % i for i in range(8)]
    lin(T.dum[:], T.dum[:], 1.0, col("pm"), ["dum", "pm"], ["dum"])
    lin(T.wb[:, BFW.index("c"), :, 0:2], T.bd[:, :, 0:2], -1.0, 0.0, ["bd", "wb_c"], ["wb_c"])
    ts(col("ws0"), col("pm"), 10.5, 0.5, A.is_lt, A.mult, ["pm"], ["ws0"])
    lin(col("ws"), oh(1), -0.5, col("ws0"), ["oh", "ws0"], ["ws"])
    lin(wb["s"], T.bd[:], col("ws"), 0.0, ["bd", "ws", "wb_s"], ["wb_s"])
    lin(col("r0"), oh2(1), K - 3.5, 0.0, ["oh2"], ["r0"])
    lin(col("r1"), oh2(2), K - 32.5, col("r0"), ["oh2", "r0"], ["r1"])
    lin(col("r3"), oh(6), K - 2048.5, col("r1"), ["oh", "r1"], ["r3"])
    lin(col("r4"), oh(7), -K + 2047.5, col("r3"), ["oh", "r3"], ["r4"])
    lin(col("r5"), oh(8), K - 2048.5, col("r4"), ["oh", "r4"], ["r5"])
    lin(col("r2"), oh(9), -K + 2047.5, col("r5"), ["oh", "r5"], ["r2"])
    lin(col("hb"), oh2(7), -MAG, 0.0, ["oh2"], ["hb"])
    lin(col("qb0"), oh2(6), V - BIG - K2, -1.0, ["oh2"], ["qb0"])
    ts(col("os"), col("pm"), 11.5, 0.5, A.is_lt, A.mult, ["pm"], ["os"])
    lin(col("ob"), col("os"), -256.0, 0.0, ["os"], ["ob"])
    lin(col("d0"), oh(1), -1.0, 1.0, ["oh"], ["d0c"])
    lin(T.d0[:], T.zero[:, 0:C], 1.0, col("d0"), ["zero", "d0c"], ["d0"])
    lin(col("t0"), oh(0), -2.5 * 2.0 ** 97, 0.0, ["oh"], ["t0"])
    scan(T.thr[:], T.half[:], T.zero[:, 0:C], col("t0"), ["half", "zero", "t0"], ["thr"])
    ts(T.lt[:], T.ki[:], col("pm"), -0.5, A.is_lt, A.mult, ["ki", "pm"], ["lt"])
    lin(T.lt[:], T.lt[:], 1.0, 1.0, ["lt"], ["lt"])
    scan(T.ww[:, 0:16], T.lt[:], T.zero[:, 0:16], 2.0 ** 96, ["lt", "zero"], ["ww0"])
    scan(T.ww[:, 16:27], T.c16[:, 0:11], T.zero[:, 0:11], T.ww[:, 15:16], ["c16", "zero", "ww0"], ["ww1"])
    ww = ["ww0", "ww1"]
    cp(T.ix0[:], T.sti[:], ["sti"], ["ix0"])
    for c, (o, m) in enumerate(CH):
        lin(T.y0[:, o:o + m], T.cxb[:, o:o + m], 2.0, 256.0, ["cxb%d" % c], ["y0_%d" % c])
    for i in range(4):
        cp(T.pool[:, BASE + lb_[i]:BASE + lb_[i + 1]], T.raw[:, lb_[i]:lb_[i + 1]], ["raw%d" % i], ["pool%d" % i])
    allpool = ["poolA", "poolB"] + ["pool%d" % i for i in range(4)]

    def store0(v):
        a, b = [(0, 2048), (2048, V)][v]
        dma("sp", T.yp[:, a:b], T.pool[:, BASE + a:BASE + b], allpool + ["PW", "PC", "i1_1"], ["yp%d" % v])

    def bank(c, i):
        return T["pb%d" % (2 * c + i)], "B%d" % (2 * c + i)

    t0, t1 = T.pb6, T.pb7

    def xpass(v, c, first, which):
        o, m = CH[c]
        p, b = bank(c, which)
        k = ("x", "x2")[which]
        arr = [["arr:y%d_a" % v], ["arr:y%d_1" % v, "arr:y%d_0" % v], ["arr:y%d_2" % v]][c] if first and v else []
        pe([(p[:, 0:m], wb[k], T["y%d" % v][:, o:o + m], True, True)], ["wb_" + k, "y%d_%d" % (v, c)] + arr, ["p%s%d" % (k, c)], [b])

    def gather(v, c, k):
        o, m = CH[c]
        src = (T["ix%d" % v], T.i1, T.i2)[k]
        if k > 0:
            r = ["i%d_%d" % (k, c)]
        elif v == 0:
            r = ["ix0"]
        else:
            r = [["arr:i%d_1" % v], ["arr:i%d_1" % v, "arr:i%d_0" % v], ["arr:i%d_2" % v]][c]
        lin(T.rec[:, o:o + m], pw.indirect(src[:, o // 16:(o + m) // 16]), col("cs1"), col("cb"), r + allpool + ["PW", "cb", "cs"], ["rec%d" % c])
        ops[-1]["lock"] = "r"

    def step(v, c, k):
        o, m = CH[c]
        (p0, b0), (p1, b1) = bank(c, 0), bank(c, 1)
        y = T["y%d" % v]
        tt(T.pr[:, o:o + m], T.rec[:, o:o + m], p0[:, 0:m], A.mult, ["rec%d" % c, "px%d" % c], ["pr%d" % c], [b0])
        tt(y[:, o:o + m], T.rec[:, o:o + m], p1[:, 0:m], A.add, ["rec%d" % c, "px2%d" % c], ["y%d_%d" % (v, c)], [b1])
        both = c > 0 and k < 2
        if both:
            xpass(v, c, False, 1)
            if c == 1:
                return
            xpass(v, c, False, 0)
            c, o, m = 1, CH[1][0], S - C
            (p0, b0), (p1, b1) = bank(c, 0), bank(c, 1)
        M, a0, na = m // 8, o // 16, m // 16
        lz, mk = T["lz%d" % c], T["mk%d" % c]
        pe([(p0[0:M, q:256:8], T.pr[:, o + q:o + m:8], T.wz[:], True, True) for q in range(8)],
           ["pr%d" % c, "wz0", "wz1", "wz2", "wz3"] + (["pr2"] if both else []), ["px%d" % c], [b0])
        if k < 2 and not both:
            xpass(v, c, False, 1)
        lin(mk[0:M, :], p0[0:M, 0:128], 400.0, 0.0, ["px%d" % c], ["mk%d" % c], [b0], f=F.Sigmoid)
        tt(lz[0:M, 1:32:2, :], mk[0:M, :], p0[0:M, 128:256], A.mult, ["mk%d" % c, "px%d" % c], ["lz%d" % c], [b0])
        lo = p1[:, 416:416 + na]
        pe([(lo, lz[0:M, 16 * (q // 2) + 1 - q % 2:16 * (q // 2) + 17 - q % 2, :], T.ih[0:M, q % 2:M:2], q == 0, q == 3) for q in range(4)],
           ["lz%d" % c, "ih"], ["lo%d" % c], [b1])
        if k < 2:
            xpass(v, c, False, 0)
        if k == 2 and v == 2 and c > 0:
            lin(T.fs[:, a0:a0 + na], lo, 1.0, 2048.0, ["lo%d" % c], ["fs%d" % c], [b1])
        else:
            dst = (T.i1, T.i2, T["io%d" % v])[k]
            nm = "i%d_%d" % (k + 1, c) if k < 2 else "io%d_%d" % (v, c)
            ts(dst[:, a0:a0 + na], lo, 2048.0, None, A.add, None, ["lo%d" % c], [nm] + (["i%d_2" % (k + 1)] if both else []), [b1])
        if c == 0 and k == 1:
            lin(T.sf[:], lo, 1.0, 0.0, ["lo0"], ["sf"], [b1])
            lin(T.el1[:], lo, 1.0, 2048.0 + BASE - 1 - BIG, ["lo0"], ["el1"], [b1])
        if c == 0 and k == 2:
            lin(T.tf[:], lo, 1.0, 0.0, ["lo0"], ["tf"], [b1])
            lin(T.el2[:, 12:24], lo, 1.0, 2048.0 + BASE - 1 - BIG, ["lo0"], ["el2b"], [b1])
            lin(T.tb[:], lo, 1.0, 2048.0 + BASE, ["lo0"], ["tb"], [b1])
        if k == 2:
            no = (416, 0, 608)[c]
            if v < 2:
                if c == 1:
                    send(1, T["y%d" % (v + 1)][:, 0:C], y[:, o:o + C], ["y%d_1" % v], "y%d_a" % (v + 1))
                    send(1, T["y%d" % (v + 1)][:, C:m], y[:, o + C:o + m], ["y%d_1" % v], "y%d_1" % (v + 1))
                else:
                    send(1, T["y%d" % (v + 1)][:, no:no + m], y[:, o:o + m], ["y%d_%d" % (v, c)], "y%d_%d" % (v + 1, c))
                if c > 0:
                    send(1, T["ix%d" % (v + 1)][:, no // 16:no // 16 + na], T["io%d" % v][:, a0:a0 + na], ["io%d_%d" % (v, c)], "i%d_%d" % (v + 1, c))
            else:
                lin(T.xo[:, o:o + m], y[:, o:o + m], col("os"), col("ob"), ["y2_%d" % c, "os", "ob"], ["xo%d" % c])
                send(-2, T.xland[:, o:o + m], T.xo[:, o:o + m], ["xo%d" % c], "xf%d" % c)
                for j, p, m1 in [[(384, 0, 192)], [(576, 192, 32), (0, 224, 384)], [(608, 608, 416)]][c]:
                    dma("sp", T.yx[:, j:j + m1], T.xland[:, p:p + m1], ["arr:xf%d" % c], [])
                if c == 2:
                    send(-2, T.fland[:, 12:64], T.fs[:, 12:64], ["fs1", "fs2"], "ff")
                    for j, p, m1 in [(36, 12, 2), (0, 14, 24), (38, 38, 26)]:
                        dma("sp", T.ys[:, j:j + m1], T.fland[:, p:p + m1], ["arr:ff"], [])

    def pick(out, win, idx, r, w):
        op("act", lambda e: e.activation(out, win.indirect(idx), F.Identity), r, w)

    def compare(row, rown, lst, lstn, wt, wtn, out, b, outn, close):
        for a in range(12):
            ts(T.eb[:, a, 16 * a:C], row[:, 16 * a:C], lst[:, a:a + 1], wt[:, a:a + 1], A.is_equal, A.mult, [rown, lstn] + wtn, ["eb%d" % a])
        for x in (range(0, 6), range(6, 12)):
            pe([(out[:, 16 * u:C], wb["c"], T.eb[:, u, 16 * u:C], False, close and u == 11) for u in x],
               ["eb%d" % u for u in x] + ["wb_c", outn], [outn], [b])

    def tolist(out, first, rhs):
        return [(out, wf["i"], first, True, False)] + [(out, T.wl[:, 15 - r:143 - r], rhs(r), False, r == 15) for r in range(16)]

    def early(v):
        s = T.i2[:, 0:12]
        ts(T.srow[:], T.ident[:, 0:W].indirect(s), -2048.0, None, A.add, None, ["i2_0"] + ids, ["srow"])
        pick(T.recs_[:], pw, s, ["i2_0", "PW", "PC"] + allpool, ["recs"])
        pe([(t0[:, 0:C], wb["c"], T.thr[:], True, False)], ["wb_c", "thr"], ["r0p"], ["B6"])
        compare(T.srow, "srow", T.sf, "sf", T.ww[:, 15:27], ww, t0, "B6", "r0p", True)
        lin(T.sg1[:], t0[:, 0:C], 1.0, 0.0, ["r0p"], ["sg1"], ["B6"], f=F.Sign)
        pe(tolist(t0[:, 192:204], T.el1[:], lambda r: T.sg1[:, r:C:16]), ["wf_i", "el1", "wl", "sg1"], ["p1"], ["B6"])
        tt(T.s1f[:], t0[:, 192:204], T.dum[:, 12:24], A.max, ["p1", "dum"], ["s1f"], ["B6"])
        cp(T.si[:, 0:12], T.s1f[:], ["s1f"], ["si0"])
        lin(T.wbig[:], t0[:, 192:204], 1e29, 0.0, ["p1"], ["wbig"], ["B6"], f=F.Relu)
        tt(T.w1[:], T.wbig[:], T.ww[:, 15:27], A.min, ["wbig"] + ww, ["w1"])
        lin(T.el2[:, 0:12], T.dum[:, 0:12], 0.0, col("lb%d" % v), ["dum", "lb%d" % v], ["el2a"])

    def stage1(v):
        r1 = t1[:, 256:448]
        pe([(r1, T.wr1[:], T.pr[:, 0:C], True, True)], ["wr1", "pr0"], ["r1p"], ["B7"])
        lin(T.sgn[:], r1, 1.0, 0.0, ["r1p"], ["sgn"], ["B7"], f=F.Sign)
        lin(T.inc[:], T.sgn[:], 1.0, 0.0, ["sgn"], ["inc"], f=F.Relu)
        pe([(t1[:, 0:C], wb["c"], T.thr[:], True, False), (t1[:, 0:C], wb["win"], T.sg1[:], False, False),
            (t1[:, 0:C], wb["sg"], T.sgn[:], False, False)], ["wb_c", "thr", "wb_win", "sg1", "wb_sg", "sgn"], ["r2p"], ["B7"])
        pe([(t1[:, 0:C], T.wsr[:], T.srow[:], False, False)], ["wsr", "srow", "r2p"], ["r2p"], ["B7"])
        pe([(t1[:, 0:C], wf["rs"], T.recs_[:], False, False)], ["wf_rs", "recs", "r2p"], ["r2p"], ["B7"])

    def scat1(v):
        tt(pall.indirect(T.si[:, 0:12]), T.recs_[:], T.inc[:], A.add, ["si0", "recs", "inc"], ["PC"])
        ops[-1]["lock"] = "w"
        pick(T.bn[:, 2 * C:], pw, T["io%d" % v][:, 0:12], ["io%d_0" % v, "PW", "PC"], ["rect"])
        pick(T.bn[:, 0:C], pall, T.si[:, 0:12], ["si0", "PW", "PC"], ["bn0"])
        if v == 2:
            for i in (14, 15):
                dma("sp", T.cnt2[i:128:16, BASE:], T.pool[i:128:16, BASE:], ["PW", "PC"], ["cnt%d" % i])

    def late(v):
        (a0, ba0), (a1, ba1) = bank(0, 0), bank(0, 1)
        ts(T.trow[:], T.ident[:, 0:W].indirect(T["io%d" % v][:, 0:12]), -2048.0, None, A.add, None, ["io%d_0" % v] + ids, ["trow"])
        compare(T.trow, "trow", T.tf, "tf", T.w1, ["w1"], t1, "B7", "r2p", False)
        pe([(t1[:, 0:C], wf["rt"], T.bn[:, 2 * C:], False, True)], ["wf_rt", "rect", "r2p"], ["r2p"], ["B7"])
        r3 = a1[:, 192:384]
        pe([(r3, wb["y"], T["y%d" % v][:, 0:C], True, False), (r3, wf["h"], T.bn[:, 2 * C:], False, True)],
           ["wb_y", "wf_h", "rect", "y%d_0" % v], ["r3p"], [ba1])
        lin(T.rr[:], r3, 1.0, MAG, ["r3p"], ["rr"], [ba1])
        lin(T.bn[:, C:2 * C], T.rr[:], 1.0, -MAG, ["rr"], ["bn1"])
        lin(T.hz[:, C:], T.rr[:], oh2(7), col("hb"), ["rr", "oh2", "hb"], ["hm"])
        lin(T.fl[:], t1[:, 0:C], 1.0, col("r2"), ["r2p", "r2"], ["fl"], ["B7"], f=F.Sign)
        pe([(t0[:, 0:C], wb["s"], T.fl[:], True, True)], ["wb_s", "fl"], ["r0p"], ["B6"])
        lin(T.cr[:, 1], t0[:, 0:C], 1.0, -2.0, ["r0p"], ["cr1"], ["B6"], f=F.Relu)
        scan(T.cr[:, 0], T.d0[:], T.cr[:, 1], 0.0, ["d0", "cr1"], ["cr0"])
        pe([(a0[:, 0:C], wb["qs"], T.sgn[:], True, False)], ["wb_qs", "sgn"], ["px0"], [ba0])
        pe([(a0[:, 0:C], wb["q"], T.cr[:, 0], False, True)], ["wb_q", "cr0", "px0"], ["px0"], [ba0])
        mm = tolist(t1[:, 204:228], T.el2[:], lambda r: T.cr[:, :, r:C:16])
        pe(mm[:1], ["wf_i", "el2a", "el2b"], ["p2"], ["B7"])
        pe(mm[1:], ["wl", "cr0", "cr1", "p2"], ["p2"], ["B7"])
        lin(T.qn[:, 0:C], a0[:, 0:C], 1.0, col("qb%d" % v), ["px0", "qb%d" % v], ["qn0"], [ba0])
        tt(T.idf[:], t1[:, 204:228], T.dum[:], A.max, ["p2", "dum"], ["idf"], ["B7"])
        cp(T.si[:, 12:36], T.idf[:], ["idf"], ["si1"])
        tt(T.ncf[:], T.idf[:, 0:12], T.tb[:], A.max, ["idf", "tb"], ["ncf"])
        if v < 2:
            ts(T["nc%d" % v][:], T.ncf[:], -float(BASE), None, A.add, None, ["ncf"], ["nc%d" % v])
            send(1, T["ix%d" % (v + 1)][:, 26:38], T["nc%d" % v][:], ["nc%d" % v], "i%d_0" % (v + 1))
            pe([(t0[:, 256:257], wb["tot"], T.cr[:, 0, C - 1:C], True, True)], ["wb_tot", "cr0"], ["totp"], ["B6"])
            lin(col("qb%d" % (v + 1)), t0[:, 256:257], oh2(6), col("qb%d" % v), ["totp", "oh2", "qb%d" % v], ["qb%d" % (v + 1)], ["B6"])
            lin(col("lb%d" % (v + 1)), t0[:, 256:257], 1.0, col("lb%d" % v), ["totp", "lb%d" % v], ["lb%d" % (v + 1)], ["B6"])
        else:
            lin(T.fs[:, 0:12], T.ncf[:], 1.0, -float(BASE), ["ncf"], ["fs0"])
            send(-2, T.fland[:, 0:12], T.fs[:, 0:12], ["fs0"], "f0")
            dma("sp", T.ys[:, 24:36], T.fland[:, 0:12], ["arr:f0"], [])
        tt(pall.indirect(T.si[:, 0:24]), T.bn[:, 0:2 * C], T.qn[:], A.max, ["si0", "si1", "bn0", "bn1", "qn0", "qn1"], ["PW", "PC"])

    for v in range(3):
        if v == 0:
            store0(0)
        for c in range(3):
            xpass(v, c, True, 0)
            xpass(v, c, True, 1)
        gather(v, 0, 0); step(v, 0, 0)
        if v > 0:
            pick(T.g2[:], pall, T.si[:, 24:36], ["si1", "PW", "PC"], ["g2"])
            tt(pall.indirect(T.si[:, 24:36]), T.g2[:], T.hz[:, C:], A.subtract, ["si1", "g2", "hm"], ["PC"])
            ops[-1]["lock"] = "w"
        gather(v, 0, 1); step(v, 0, 1)
        early(v)
        gather(v, 0, 2); step(v, 0, 2)
        stage1(v)
        for k in range(3):
            for c in (1, 2):
                gather(v, c, k); step(v, c, k)
            if k == 0 and v == 1:
                store0(v)
        scat1(v)
        late(v)
    tt(T.cnt2[:, 0:BASE + W].indirect(T.si[:, 12:36]), T.bn[:, C:], T.hz[:], A.subtract, ["si1", "bn1", "rect", "hm", "hz0", "cnt14", "cnt15"], ["cnt"])
    yps = ["yp0", "yp1"]
    for i in range(8):
        dma("act" if i % 2 else "sp", T.yp[16 * i:16 * i + 12, V:W], T.pool[16 * i:16 * i + 12, BASE + V:], ["PW", "PC"], [])
    for i in (12, 13):
        dma("sp" if i == 12 else "act", T.yp[i:128:16, :], T.pool[i:128:16, BASE:], ["PW", "PC"] + yps, [])
    for i in (14, 15):
        dma("sp" if i == 14 else "act", T.yp[i:128:16, :], T.cnt2[i:128:16, BASE:], ["cnt"] + yps, [])
    return ops


def edges(ops):
    lastw, readers, bk, deps = {}, {}, {}, []
    for i, o in enumerate(ops):
        d = {}
        for x in o["r"]:
            if x in lastw:
                d[lastw[x]] = True
        for x in o["w"]:
            for j in ([lastw[x]] if x in lastw else []) + readers.get(x, []):
                d[j] = True
        for b in o["banks"]:
            for e2, j in bk.setdefault(b, {}).items():
                d[j] = d.get(j, False) or e2 != o["eng"]
            bk[b][o["eng"]] = i
        for j in list(d):
            if ops[j]["eng"] == "pe" and o["eng"] == "pe":
                d[j] = False
        d.pop(i, None)
        deps.append(d)
        for x in o["r"]:
            if not (o["kind"] == "dma" and x == "i1_1"):
                readers.setdefault(x, []).append(i)
        for x in o["w"]:
            lastw[x] = i
            readers[x] = []
    return deps


def waits(ops, deps, order):
    pos, cnt = {}, {}
    for i in order:
        if ops[i]["kind"] == "c":
            cnt[ops[i]["eng"]] = cnt.get(ops[i]["eng"], 0) + 1
            pos[i] = cnt[ops[i]["eng"]]
    rank = {i: k for k, i in enumerate(order)}
    known, clock, need = {}, {}, {}
    for i in order:
        kn = known.setdefault(ops[i]["eng"], {})
        need[i] = []
        for j in sorted([j for j in deps[i] if deps[i][j]], key=lambda j: -rank[j]):
            key, val = (ops[j]["eng"], pos[j]) if ops[j]["kind"] == "c" else (ops[j]["sem"], 1)
            if kn.get(key, 0) >= val:
                continue
            need[i].append(j)
            for k2, v2 in clock[j].items():
                kn[k2] = max(kn.get(k2, 0), v2)
        if ops[i]["kind"] == "c":
            clock[i] = dict(kn); clock[i][ops[i]["eng"]] = pos[i]
        elif ops[i]["kind"] == "dma":
            clock[i] = dict(kn); clock[i][ops[i]["sem"]] = 1
        else:
            clock[i] = {ops[i]["sem"]: 1}
    return need


ORDER = "05060i0n07040m00010x02030h0e1o0k1p0f1q1s0y0b2e291t221b1r0g0917251u2z2b1v0u330a0d0q081w2t300c2d0o2f3121320v0l2i2a0j240p232c370w2x1j2g2h18342s1k4r203d1y2l1x192r1z2m272y2u1n382v462n2w1a2o2j0r2k2p281l2q0s391m0t1g3c3a1e3b3i1h361f3j1i3k5e3l1c3g153m1d3h3n165f35110z3o5a5g3p12103e3r26133q3s3f5b145h3t5i3u3v5c5j3x3w3y5k5d3z5l40415m5n42444s5o5t494i4a4t4d4c4b4v4h4754485p4g4e4f4j5v5u4k55435w4l5r5x4w564u4m4x455q534y4n5s4o4p4z5y6p505157525z58594q606q6s616r62636t786x646u726v6w746y717g736z75706f667665776c796g7a676d7c6h686i7b7d696j7i6n7e6a6k6b6l7f6e7j6m6o7q7h7l7r7k7m7n7s7o7t7p8q9b7u7v7w7x809y8182837y859u7z869z8884a0878a899va18ca29wa38d9x8ea4a58f8g8b8ha6a78ia88ja9ae8k8l8o8m9c928r908t8n8uaa8v918s8w8z8y8x939daf8p9o94ab9p9f959eajac9g9n9q96ak9hagal9i97ad98999jamba9kc19lan9m9rao9sbdap9t9abiaibebgbhahbbbfbjbkaqbqb0bpboblasbmbnarbratbcbsb1axaubtb2bxaybyb8buavc3bzawb3bvazc0bwc4b4b5c2c6b6c5cbc7b7cecccdb9dbdwcgcfcic8chclc9cacvcmcncocwcpcqckcjcrelcsctcucxenczeheocyemd1d0d2eiepd3ejeqd4erd5d6ekesdad9eteud7dxevdfdhdgdcf0dedidddjdkdmdodndydlewf2e0dpf1f3dqebeyd8e1f4ecdrdze2edexe8eze9dsf5dtdug2gvf6e3eeeff7egdvg4g5e4g6g7f8g3f9fae5e6fbgig8gbgagdg9gcgggegfgkfnghgjfdglfceae7gmfjfpgngrfkfofvgsgxgtfqfwgofegufrgygqfsffgpfggwh0ftgzfhh2h1fufih6h3fyh4h7hchhhghdhehfhahbfmh9flh8fxhjhig1fzg0h5"


def rank_program(g, core, T, topo):
    if T.rank_of(core) is None:
        return
    ops = build(T, topo, core)
    deps = edges(ops)
    order = [int(ORDER[i:i + 2], 36) for i in range(0, len(ORDER), 2)]
    seen = {"r": [], "w": []}
    for i in order:
        k = ops[i]["lock"]
        if k:
            for j in seen["w" if k == "r" else "r"]:
                deps[i][j] = True
            seen[k].append(i)
    need = waits(ops, deps, order)
    q = {"pe": g.tensor, "act": g.scalar, "dve": g.vector, "g": g, "sp": g.sync}
    marked = set(j for i in order for j in need[i])
    val, cnt, sent = {}, {}, 0
    for i in order:
        o = ops[i]
        e = q[o["eng"]]
        for j in need[i]:
            if ops[j]["kind"] == "c":
                e.wait_ge(T.sem["c_" + ops[j]["eng"]], val[j])
            else:
                e.wait_ge(T.sem[ops[j]["sem"]], ops[j]["inc"])
        ins = o["fn"](e)
        if o["kind"] == "c":
            if i in marked:
                cnt[o["eng"]] = cnt.get(o["eng"], 0) + 1
                val[i] = cnt[o["eng"]]
                ins.then_inc(T.sem["c_" + o["eng"]], 1)
        elif o["kind"] == "dma":
            ins.then_inc(T.sem[o["sem"]], 16)
        else:
            sent += o["loc"]
    g.wait_ge(T.sem.sent, sent)
    for i in order:
        if ops[i]["kind"] == "dma" and i not in marked:
            g.sync.wait_ge(T.sem[ops[i]["sem"]], 16)
